import numpy as np
import ml_dtypes


def mxq(x, axis, fmt="e4m3"):
    dtype, down = {"e4m3": (ml_dtypes.float8_e4m3fn, 7), "e5m2": (ml_dtypes.float8_e5m2, 14)}[fmt]
    v = np.moveaxis(np.asarray(x, np.float32).astype(ml_dtypes.bfloat16).astype(np.float64), axis, -1)
    blocks = v.reshape(v.shape[:-1] + (-1, 32))
    amax = np.abs(blocks).max(-1, keepdims=True)
    byte = np.maximum(np.where(amax > 0, np.frexp(amax)[1] - 1 + 127, 0) - down, 1)
    scale = np.exp2(byte - 127.0)
    codes = (blocks / scale).astype(np.float32).astype(dtype).astype(np.float64)
    return np.moveaxis((codes * scale).reshape(v.shape), -1, axis)


WIDE = False


def mx_kscale(k):
    if not WIDE:
        return np.ones(k)
    levels = np.array([24, -24, 12, -12, 0])
    if k % 512:
        return np.exp2(np.random.permutation(np.resize(levels, k // 32))).repeat(32)
    a = np.empty((k // 512, 16))
    for p in range(k // 512):
        a[p, :8] = np.random.permutation(np.resize(levels, 8))
        for g in range(8):
            far = levels[np.abs(levels - a[p, g]) >= 10]
            a[p, g + 8] = far[np.random.randint(len(far))]
    return np.exp2(a.ravel()).repeat(32)


def f64(x):
    return np.asarray(x).astype(np.float64)


def striped(idx):
    return np.tile(idx.reshape(-1, 16).T, (8, 1)).astype(np.uint16)


def unstriped(offs):
    return offs[:16].T.reshape(-1).astype(np.int64)


E2M1 = np.array([0.0, 0.5, 1.0, 1.5, 2.0, 3.0, 4.0, 6.0, -0.0, -0.5, -1.0, -1.5, -2.0, -3.0, -4.0, -6.0])


def pack_weight(w, fmt):
    k, n = w.shape
    w = f64(np.asarray(w, np.float32).astype(ml_dtypes.bfloat16)).reshape(k // 32, 32, n)
    amax = np.abs(w).max(1)
    if fmt == "e4m3":
        byte = np.frexp(amax)[1] - 1 + 127 - 7
    else:
        mant, ex = np.frexp(amax / 6.0)
        byte = np.where(mant > 0.5, ex, ex - 1) + 127
    byte = np.clip(np.where(amax > 0, byte, 1), 1, 254)
    scaled = (w * np.exp2(127.0 - byte)[:, None, :]).reshape(k, n).astype(np.float32)
    by_word = np.ascontiguousarray(scaled.reshape(k // 512, 128, 4, n).transpose(0, 1, 3, 2))
    if fmt == "e4m3":
        words = by_word.astype(ml_dtypes.float8_e4m3fn).view(np.uint8)
    else:
        c = by_word.astype(ml_dtypes.float4_e2m1fn).view(np.uint8) & 0xF
        words = (c[..., 0::2] | (c[..., 1::2] << 4)).reshape(k // 512, 128, 2 * n)
    return np.ascontiguousarray(words), np.ascontiguousarray(byte.astype(np.uint8).reshape(k // 512, 16, n))


def unpack_weight(words, scales, fmt):
    g, _, n = scales.shape
    words = np.ascontiguousarray(words).reshape(g, 128, n, -1)
    if fmt == "e4m3":
        vals = words.view(ml_dtypes.float8_e4m3fn).astype(np.float64)
    else:
        nib = np.empty((g, 128, n, 4), np.uint8)
        nib[..., 0::2] = words & 0xF
        nib[..., 1::2] = words >> 4
        vals = E2M1[nib]
    vals = vals * np.repeat(np.exp2(scales.astype(np.float64) - 127.0), 8, axis=1)[..., None]
    return vals.transpose(0, 1, 3, 2).reshape(g * 512, n)


def planes(y):
    n, m = y.shape
    v = y.astype(np.float32).astype(ml_dtypes.bfloat16).astype(np.float64).reshape(n // 32, 32, m)
    top = np.abs(v).max(1)
    byte = np.clip(np.where(top > 0, np.frexp(top)[1] - 1 + 127 - 7, 1), 1, 254)
    codes = (v * np.exp2(127.0 - byte)[:, None, :]).reshape(n, m).astype(np.float32).astype(ml_dtypes.float8_e4m3fn).view(np.uint8)
    words = codes.reshape(n // 512, 128, 4, m).transpose(0, 1, 3, 2)
    return np.ascontiguousarray(words), np.ascontiguousarray(byte.astype(np.uint8).reshape(n // 512, 16, m))


def silu(f):
    return f / (1.0 + np.exp(-np.maximum(f, -700.0)))


K, R, N, T, J = 1024, 512, 512, 2048, 1024


def setup_inputs():
    n = np.random.standard_normal
    s = mx_kscale(K)[:, None]
    u = mx_kscale(R)[:, None]
    wd = n((R, N)) / np.sqrt(R) / u
    wd4 = pack_weight(wd, "e2m1")
    wdrest = wd - unpack_weight(*wd4, "e2m1")
    p_tab = pack_weight(n((K, T)) * s, "e4m3")
    p_wd8 = pack_weight(wdrest, "e4m3")
    return {
        "tab_words": p_tab[0],
        "tab_scales": p_tab[1],
        "wu": (n((K, R)) / np.sqrt(K) / s).astype(np.float32),
        "sm": (np.random.uniform(0.5, 2.0, R) * u[:, 0]).astype(np.float32),
        "wd4_words": wd4[0],
        "wd4_scales": wd4[1],
        "wd8_words": p_wd8[0],
        "wd8_scales": p_wd8[1],
        "rT": (n((N, T))).astype(np.float32),
        "b": (0.3 * n(N)).astype(np.float32),
        "wgo": np.tile(np.random.uniform(0.5, 2.0, J), (128, 1)).astype(np.float32),
        "offs": striped(np.random.permutation(T)[:J]),
    }


def reference(tab_words, tab_scales, wu, sm, wd4_words, wd4_scales, wd8_words, wd8_scales, rT, b, wgo, offs):
    idx = unstriped(offs)
    tab_ = unpack_weight(tab_words, tab_scales, "e4m3")[:, idx]
    wu_ = mxq(f64(wu), 0, "e4m3")
    a = wu_.T @ tab_
    h = f64(sm)[:, None] * silu(a)
    h_ = mxq(h, 0, "e4m3")
    wd4_ = unpack_weight(wd4_words, wd4_scales, "e2m1")
    wd8_ = unpack_weight(wd8_words, wd8_scales, "e4m3")
    y = wd4_.T @ h_ + wd8_.T @ h_
    out = np.zeros((N, T))
    out[:, idx] = f64(wgo)[0] * (y + f64(rT)[:, idx] + f64(b)[:, None])
    return (out,) + planes(out)

@@ -1,0 +1,307 @@
+from contextlib import ExitStack
+
+import concourse.mybir as mybir
+
+K, R, N, T, J = 1024, 512, 512, 2048, 1024
+FLOPS = 2 * K * R * J + 2 * 2 * R * N * J
+
+F32 = mybir.dt.float32
+BF16 = mybir.dt.bfloat16
+I32 = mybir.dt.int32
+U32 = mybir.dt.uint32
+U16 = mybir.dt.uint16
+U8 = mybir.dt.uint8
+FP8X4 = mybir.dt.float8_e4m3fn_x4
+FP4X4 = mybir.dt.float4_e2m1fn_x4
+ACT = mybir.ActivationFunctionType
+ADD = mybir.AluOpType.add
+MULT = mybir.AluOpType.mult
+
+P = 128
+PACK = 4
+BANK = 512
+NARROW = 128
+SLICE_ORDER = (2, 0, 1, 3)
+BLOCK = 512
+VECTOR_SHARE = 256
+
+
+def tile_list_modp_silu_res_resbP_kernel(
+    tc, tab_words, tab_scales, wu, sm, wd4_words, wd4_scales, wd8_words, wd8_scales, rT, b, wgo, offs,
+    out_0, out_1, out_2,
+):
+    nc = tc.nc
+    with ExitStack() as ctx:
+        keep = ctx.enter_context(tc.tile_pool(name="keep", bufs=1))
+        psum = ctx.enter_context(tc.psum_pool(name="psum", bufs=8))
+
+        def sb(name, shape, dtype, tag=""):
+            return keep.tile(shape, dtype, name=name, tag=tag or name, align_bytes=64)
+
+        offsets = keep.tile([P, J // 16], U16, name="offsets")
+        nc.sync.dma_start(offsets[:], offs)
+
+        def listed(j0, j1):
+            return offsets[:, j0 // 16 : j1 // 16]
+
+        tab_sc = sb("tab_sc", [P, T], U8)
+        nc.vector.memset(tab_sc[:].bitcast(I32), 0)
+        wd_sc_raw = sb("wd_sc_raw", [P, N], U8)
+        nc.gpsimd.memset(wd_sc_raw[:].bitcast(I32), 0)
+        warm_in = sb("warm_in", [P, 1], F32)
+        warm_out = sb("warm_out", [P, 1], F32)
+        nc.gpsimd.memset(warm_in[:], 0.0)
+        nc.scalar.activation(warm_out[:], warm_in[:], ACT.Silu)
+
+        for q in range(4):
+            nc.scalar.dma_start(
+                out=tab_sc[32 * q : 32 * q + 8, :].bitcast(I32),
+                in_=tab_scales[:, 4 * q : 4 * q + 4, :].bitcast(I32),
+            )
+
+        wu_rows = [wu[512 * a : 512 * (a + 1), :].rearrange("(p i) r -> p i r", i=PACK) for a in range(2)]
+        tab_w = [sb("tab_w%d" % a, [P, T], I32) for a in range(2)]
+        wu_parts = [(0, 0, R), (1, 0, R // 2), (1, R // 2, R)]
+        wu_raw = [sb("wu_raw%d" % u, [P, PACK, r1 - r0], F32) for u, (a, r0, r1) in enumerate(wu_parts)]
+
+        def load_table(a):
+            nc.sync.dma_start(out=tab_w[a][:], in_=tab_words[a].rearrange("p t i -> p (t i)").bitcast(I32))
+
+        def load_wu(u):
+            a, r0, r1 = wu_parts[u]
+            nc.sync.dma_start(out=wu_raw[u][:], in_=wu_rows[a][:, :, r0:r1])
+
+        load_wu(0)
+        load_table(0)
+        load_wu(1)
+        load_wu(2)
+        load_table(1)
+        wd8_raw = sb("wd8_raw", [P, N], I32)
+        nc.sync.dma_start(out=wd8_raw[:], in_=wd8_words[0].rearrange("p n i -> p (n i)").bitcast(I32))
+        wd4_raw = sb("wd4_raw", [P, 2 * N], U8)
+        nc.sync.dma_start(out=wd4_raw[:].bitcast(I32), in_=wd4_words[0].bitcast(I32))
+        sm_sb = sb("sm_sb", [P, PACK], F32)
+        nc.sync.dma_start(out=sm_sb[:], in_=sm.rearrange("(p t) -> p t", t=PACK))
+        b_sb = sb("b_sb", [P, PACK], F32)
+        nc.sync.dma_start(out=b_sb[:], in_=b.rearrange("(p t) -> p t", t=PACK))
+        res = {t: sb("res%d" % t, [P, T], F32) for t in SLICE_ORDER}
+        res_rows = rT.rearrange("(p t) c -> p t c", t=PACK)
+        nc.sync.dma_start(out=res[SLICE_ORDER[0]][:], in_=res_rows[:, SLICE_ORDER[0], :])
+        wgo_sb = sb("wgo_sb", [P, J], F32)
+        nc.sync.dma_start(out=wgo_sb[:], in_=wgo)
+        for t in SLICE_ORDER[1:]:
+            nc.sync.dma_start(out=res[t][:], in_=res_rows[:, t, :])
+
+        for tier, scales in enumerate((wd4_scales, wd8_scales)):
+            for q in range(4):
+                row = 32 * q + 4 * tier
+                nc.gpsimd.dma_start(
+                    out=wd_sc_raw[row : row + 4, :].bitcast(I32),
+                    in_=scales[0, 4 * q : 4 * q + 4, :].bitcast(I32),
+                )
+
+        page = {t: sb("page%d" % t, [P, T], F32) for t in SLICE_ORDER}
+        for t in SLICE_ORDER:
+            nc.vector.memset(page[t][:], 0.0)
+
+        wu_bf = [sb("wu_bf%d" % a, [P, PACK, P, PACK], BF16) for a in range(2)]
+        wu_q = [sb("wu_q%d" % a, [P, R], U32) for a in range(2)]
+        wu_s = [sb("wu_s%d" % a, [P, R], U8) for a in range(2)]
+
+        def round_wu(u):
+            a, r0, r1 = wu_parts[u]
+            nc.scalar.copy(
+                out=wu_bf[a][:, :, r0 // PACK : r1 // PACK, :].rearrange("p t m i -> p m t i"),
+                in_=wu_raw[u][:].rearrange("p i (m t) -> p m t i", t=PACK),
+            )
+
+        def quantise_wu(a):
+            nc.vector.quantize_mx(
+                out=wu_q[a][:].bitcast(FP8X4), scales=wu_s[a][:],
+                in_=wu_bf[a][:].rearrange("p t m i -> p (t m i)"),
+            )
+
+        got_sc = sb("got_sc", [P, J], U8)
+        got_w = [sb("got_w%d" % a, [P, J], U32) for a in range(2)]
+
+        def gather_words(a, j0, j1):
+            nc.vector.tensor_copy(got_w[a][:, j0:j1], tab_w[a][:].bitcast(U32).indirect(listed(j0, j1)))
+
+        def up_pass(out, a, t, j0, j1, start, stop):
+            nc.tensor.matmul_mx(
+                out=out,
+                lhsT=wu_q[a][:, t * P : (t + 1) * P].bitcast(FP8X4),
+                lhsT_scale=wu_s[a][:, t * P : (t + 1) * P],
+                rhs=got_w[a][:, j0:j1].bitcast(FP8X4),
+                rhs_scale=got_sc[4 * a : P, j0:j1],
+                start=start, stop=stop,
+            )
+
+        nc.vector.tensor_copy(got_sc[:], tab_sc[:].indirect(offsets[:]))
+        round_wu(0)
+        gather_words(0, 0, J // 2)
+        quantise_wu(0)
+        gather_words(0, J // 2, J)
+        half = J // 2
+        narrow = [psum.tile([P, PACK, NARROW], F32, name="narrow%d" % c, tag="bank") for c in range(half // NARROW)]
+        wide = [psum.tile([P, BANK], F32, name="wide%d" % t, tag="bank") for t in range(PACK)]
+        for c in range(half // NARROW):
+            for t in range(PACK):
+                up_pass(narrow[c][:, t, :], 0, t, c * NARROW, (c + 1) * NARROW, t == 0, False)
+        for t in range(PACK):
+            up_pass(wide[t][:], 0, t, half, J, True, False)
+        round_wu(1)
+        round_wu(2)
+        quantise_wu(1)
+
+        h_q = [sb("h_q%d" % u, [P, half], U32) for u in range(2)]
+        h_s = [sb("h_s%d" % u, [P, half], U8) for u in range(2)]
+        act = [sb("act%d" % c, [P, NARROW, PACK], F32) for c in range(half // NARROW)]
+        h_bf = [sb("h_bf%d" % c, [P, NARROW, PACK], BF16) for c in range(half // NARROW)]
+
+        def hidden_narrow(c):
+            j0, j1 = c * NARROW, (c + 1) * NARROW
+            for t in range(PACK):
+                up_pass(narrow[c][:, t, :], 1, t, j0, j1, False, t == PACK - 1)
+            nc.scalar.activation(act[c][:], narrow[c][:].rearrange("p t j -> p j t"), ACT.Silu)
+            nc.vector.tensor_tensor(
+                h_bf[c][:], act[c][:], sm_sb[:].unsqueeze(1).to_broadcast([P, NARROW, PACK]), MULT
+            )
+            nc.vector.quantize_mx(
+                out=h_q[0][:, j0:j1].bitcast(FP8X4), scales=h_s[0][:, j0:j1],
+                in_=h_bf[c][:].rearrange("p j t -> p (j t)"),
+            )
+
+        wd8 = sb("wd8", [P, N], I32)
+        wd4 = sb("wd4", [P, 2 * N], U8)
+        wd_sc = sb("wd_sc", [P, N], U8)
+
+        def deal_wd():
+            nc.vector.tensor_copy(
+                wd8[:].rearrange("p (t m) -> p m t", t=PACK), wd8_raw[:].rearrange("p (m t) -> p m t", t=PACK)
+            )
+            nc.vector.tensor_copy(
+                wd4[:].rearrange("p (t m e) -> p m t e", t=PACK, e=2),
+                wd4_raw[:].rearrange("p (m t e) -> p m t e", t=PACK, e=2),
+            )
+            nc.vector.tensor_copy(
+                wd_sc[:].rearrange("p (t m) -> p m t", t=PACK), wd_sc_raw[:].rearrange("p (m t) -> p m t", t=PACK)
+            )
+
+        def down(t, j0, j1, y_out):
+            u = j0 // half
+            width = j1 - j0
+            step = BANK if width == BANK else NARROW
+            bank = psum.tile([P, width], F32, name="down", tag="bank")
+            for c0 in range(0, width, step):
+                cols = slice(j0 - u * half + c0, j0 - u * half + c0 + step)
+                nc.tensor.matmul_mx(
+                    out=bank[:, c0 : c0 + step],
+                    lhsT=wd4[:, 2 * t * P : 2 * (t + 1) * P].bitcast(FP4X4),
+                    lhsT_scale=wd_sc[:, t * P : (t + 1) * P],
+                    rhs=h_q[u][:, cols].bitcast(FP8X4), rhs_scale=h_s[u][:, cols],
+                    start=True, stop=False,
+                )
+                nc.tensor.matmul_mx(
+                    out=bank[:, c0 : c0 + step],
+                    lhsT=wd8[:, t * P : (t + 1) * P].bitcast(FP8X4),
+                    lhsT_scale=wd_sc[4:P, t * P : (t + 1) * P],
+                    rhs=h_q[u][:, cols].bitcast(FP8X4), rhs_scale=h_s[u][:, cols],
+                    start=False, stop=True,
+                )
+            nc.scalar.activation(y_out, bank[:], ACT.Identity, bias=b_sb[:, t : t + 1])
+
+        quarter = J // 4
+        gather_words(1, 0, quarter)
+        deal_wd()
+        hidden_narrow(0)
+        hidden_narrow(1)
+        gather_words(1, quarter, half)
+        gather_words(1, half, J)
+
+        first, second, third, last = SLICE_ORDER
+        y_sb = {t: sb("y_sb%d" % t, [P, J], F32) for t in SLICE_ORDER}
+        for t in (first, second):
+            down(t, 0, quarter, y_sb[t][:, 0:quarter])
+        hidden_narrow(2)
+        hidden_narrow(3)
+        for t in (first, second):
+            down(t, quarter, half, y_sb[t][:, quarter:half])
+
+        act_wide = sb("act_wide", [P, PACK, half], F32)
+        h_planes = sb("h_planes", [P, PACK, half], BF16)
+        h_wide = sb("h_wide", [P, half, PACK], BF16)
+        for t in range(PACK):
+            up_pass(wide[t][:], 1, t, half, J, False, True)
+            nc.scalar.activation(act_wide[:, t, :], wide[t][:], ACT.Silu)
+            nc.scalar.activation(h_planes[:, t, :], act_wide[:, t, :], ACT.Copy, scale=sm_sb[:, t : t + 1])
+        nc.scalar.copy(
+            out=h_wide[:].rearrange("p (c i) t -> p c t i", i=4),
+            in_=h_planes[:].rearrange("p t (c i) -> p c t i", i=4),
+        )
+        nc.vector.quantize_mx(
+            out=h_q[1][:].bitcast(FP8X4), scales=h_s[1][:], in_=h_wide[:].rearrange("p j t -> p (j t)")
+        )
+        for t in (first, second):
+            down(t, half, J, y_sb[t][:, half:J])
+        for t in (third, last):
+            down(t, 0, half, y_sb[t][:, 0:half])
+            down(t, half, J, y_sb[t][:, half:J])
+
+        out_rows = out_0.rearrange("(p t) c -> p t c", t=PACK)
+        woven = [sb("woven%d" % g, [P, BLOCK, PACK], BF16) for g in range(T // BLOCK)]
+        ring = sb("ring", [P, 2, J], F32)
+        units = [(t, j0, j1) for j0, j1 in ((0, quarter), (quarter, half), (half, J)) for t in (first, second)]
+        units = units + [(third, 0, J), (last, 0, J)]
+
+        sums = {}
+
+        def add_residual(k):
+            t, j0, j1 = units[k]
+            if t == last:
+                sums[k] = sb("last_sum", [P, J], F32, tag="page%d" % first)[:]
+            else:
+                sums[k] = ring[:, k % 2, 0 : j1 - j0]
+            nc.vector.tensor_tensor(sums[k], res[t][:].indirect(listed(j0, j1)), y_sb[t][:, j0:j1], ADD)
+
+        def scatter(k):
+            t, j0, j1 = units[k]
+            nc.vector.tensor_tensor(
+                page[t][:].indirect(listed(j0, j1)), sums[k], wgo_sb[:, j0:j1], MULT
+            )
+            if j1 == J:
+                nc.sync.dma_start(out=out_rows[:, t, :], in_=page[t][:])
+                if t != last:
+                    for g in range(T // BLOCK):
+                        nc.scalar.copy(out=woven[g][:, :, t], in_=page[t][:, g * BLOCK : (g + 1) * BLOCK])
+
+        add_residual(0)
+        for k in range(len(units)):
+            if k + 1 < len(units):
+                add_residual(k + 1)
+            scatter(k)
+
+        out_q = [sb("out_q%d" % g, [P, BLOCK], I32) for g in range(T // BLOCK)]
+        out_s = sb("out_s", [P, T], U8)
+        words_out = out_1[0].rearrange("p t i -> p (t i)").bitcast(I32)
+
+        def weave_last(g):
+            c0 = g * BLOCK
+            nc.vector.tensor_copy(woven[g][:, 0:VECTOR_SHARE, last], page[last][:, c0 : c0 + VECTOR_SHARE])
+            nc.scalar.copy(out=woven[g][:, VECTOR_SHARE:BLOCK, last], in_=page[last][:, c0 + VECTOR_SHARE : c0 + BLOCK])
+
+        weave_last(0)
+        for g in range(T // BLOCK):
+            if g + 1 < T // BLOCK:
+                weave_last(g + 1)
+            cols = slice(g * BLOCK, (g + 1) * BLOCK)
+            nc.vector.quantize_mx(
+                out=out_q[g][:].bitcast(FP8X4), scales=out_s[:, cols],
+                in_=woven[g][:].rearrange("p c t -> p (c t)"),
+            )
+            nc.sync.dma_start(out=words_out[:, cols], in_=out_q[g][:])
+        for q in range(4):
+            queue = nc.scalar if q % 2 else nc.sync
+            queue.dma_start(
+                out=out_2[0, 4 * q : 4 * q + 4, :].bitcast(I32), in_=out_s[32 * q : 32 * q + 4, :].bitcast(I32)
+            )

@@ -22,8 +22,8 @@ PACK = 4
 BANK = 512
 NARROW = 128
 SLICE_ORDER = (2, 0, 1, 3)
-BLOCK = 512
-VECTOR_SHARE = 256
+BLOCKS = ((0, 512), (512, 1024), (1024, 1536), (1536, 2048))
+STORES = BLOCKS
 
 
 def tile_list_modp_silu_res_resbP_kernel(
@@ -33,7 +33,7 @@ def tile_list_modp_silu_res_resbP_kernel(
     nc = tc.nc
     with ExitStack() as ctx:
         keep = ctx.enter_context(tc.tile_pool(name="keep", bufs=1))
-        psum = ctx.enter_context(tc.psum_pool(name="psum", bufs=8))
+        psum = ctx.enter_context(tc.psum_pool(name="psum", bufs=1))
 
         def sb(name, shape, dtype, tag=""):
             return keep.tile(shape, dtype, name=name, tag=tag or name, align_bytes=64)
@@ -45,23 +45,17 @@ def tile_list_modp_silu_res_resbP_kernel(
             return offsets[:, j0 // 16 : j1 // 16]
 
         tab_sc = sb("tab_sc", [P, T], U8)
-        nc.vector.memset(tab_sc[:].bitcast(I32), 0)
-        wd_sc_raw = sb("wd_sc_raw", [P, N], U8)
+        nc.gpsimd.memset(tab_sc[:].bitcast(I32), 0)
+        wd_sc_raw = sb("wd_sc_raw", [P, 2 * N], U8)
         nc.gpsimd.memset(wd_sc_raw[:].bitcast(I32), 0)
         warm_in = sb("warm_in", [P, 1], F32)
         warm_out = sb("warm_out", [P, 1], F32)
         nc.gpsimd.memset(warm_in[:], 0.0)
         nc.scalar.activation(warm_out[:], warm_in[:], ACT.Silu)
 
-        for q in range(4):
-            nc.scalar.dma_start(
-                out=tab_sc[32 * q : 32 * q + 8, :].bitcast(I32),
-                in_=tab_scales[:, 4 * q : 4 * q + 4, :].bitcast(I32),
-            )
-
         wu_rows = [wu[512 * a : 512 * (a + 1), :].rearrange("(p i) r -> p i r", i=PACK) for a in range(2)]
         tab_w = [sb("tab_w%d" % a, [P, T], I32) for a in range(2)]
-        wu_parts = [(0, 0, R), (1, 0, R // 2), (1, R // 2, R)]
+        wu_parts = [(a, r0, r0 + R // 2) for a in range(2) for r0 in (0, R // 2)]
         wu_raw = [sb("wu_raw%d" % u, [P, PACK, r1 - r0], F32) for u, (a, r0, r1) in enumerate(wu_parts)]
 
         def load_table(a):
@@ -71,19 +65,29 @@ def tile_list_modp_silu_res_resbP_kernel(
             a, r0, r1 = wu_parts[u]
             nc.sync.dma_start(out=wu_raw[u][:], in_=wu_rows[a][:, :, r0:r1])
 
-        load_wu(0)
         load_table(0)
-        load_wu(1)
-        load_wu(2)
-        load_table(1)
+        for q in range(4):
+            nc.sync.dma_start(
+                out=tab_sc[32 * q : 32 * q + 8, :].bitcast(I32),
+                in_=tab_scales[:, 4 * q : 4 * q + 4, :].bitcast(I32),
+            )
+        for u in range(len(wu_parts)):
+            load_wu(u)
         wd8_raw = sb("wd8_raw", [P, N], I32)
         nc.sync.dma_start(out=wd8_raw[:], in_=wd8_words[0].rearrange("p n i -> p (n i)").bitcast(I32))
         wd4_raw = sb("wd4_raw", [P, 2 * N], U8)
         nc.sync.dma_start(out=wd4_raw[:].bitcast(I32), in_=wd4_words[0].bitcast(I32))
+        for tier, (scales, queue) in enumerate(((wd4_scales, nc.gpsimd), (wd8_scales, nc.sync))):
+            for q in range(4):
+                queue.dma_start(
+                    out=wd_sc_raw[32 * q : 32 * q + 4, tier * N : (tier + 1) * N].bitcast(I32),
+                    in_=scales[0, 4 * q : 4 * q + 4, :].bitcast(I32),
+                )
+        load_table(1)
         sm_sb = sb("sm_sb", [P, PACK], F32)
         nc.sync.dma_start(out=sm_sb[:], in_=sm.rearrange("(p t) -> p t", t=PACK))
         b_sb = sb("b_sb", [P, PACK], F32)
-        nc.sync.dma_start(out=b_sb[:], in_=b.rearrange("(p t) -> p t", t=PACK))
+        nc.gpsimd.dma_start(out=b_sb[:], in_=b.rearrange("(p t) -> p t", t=PACK))
         res = {t: sb("res%d" % t, [P, T], F32) for t in SLICE_ORDER}
         res_rows = rT.rearrange("(p t) c -> p t c", t=PACK)
         nc.sync.dma_start(out=res[SLICE_ORDER[0]][:], in_=res_rows[:, SLICE_ORDER[0], :])
@@ -92,17 +96,9 @@ def tile_list_modp_silu_res_resbP_kernel(
         for t in SLICE_ORDER[1:]:
             nc.sync.dma_start(out=res[t][:], in_=res_rows[:, t, :])
 
-        for tier, scales in enumerate((wd4_scales, wd8_scales)):
-            for q in range(4):
-                row = 32 * q + 4 * tier
-                nc.gpsimd.dma_start(
-                    out=wd_sc_raw[row : row + 4, :].bitcast(I32),
-                    in_=scales[0, 4 * q : 4 * q + 4, :].bitcast(I32),
-                )
-
-        page = {t: sb("page%d" % t, [P, T], F32) for t in SLICE_ORDER}
-        for t in SLICE_ORDER:
-            nc.vector.memset(page[t][:], 0.0)
+        page = {t: sb("page%d" % t, [P, T], F32) for t in SLICE_ORDER[:2]}
+        for t in SLICE_ORDER[:2]:
+            nc.vector.memset(page[t][:].bitcast(I32), 0)
 
         wu_bf = [sb("wu_bf%d" % a, [P, PACK, P, PACK], BF16) for a in range(2)]
         wu_q = [sb("wu_q%d" % a, [P, R], U32) for a in range(2)]
@@ -122,77 +118,110 @@ def tile_list_modp_silu_res_resbP_kernel(
             )
 
         got_sc = sb("got_sc", [P, J], U8)
-        got_w = [sb("got_w%d" % a, [P, J], U32) for a in range(2)]
+        got_w = {}
 
-        def gather_words(a, j0, j1):
-            nc.vector.tensor_copy(got_w[a][:, j0:j1], tab_w[a][:].bitcast(U32).indirect(listed(j0, j1)))
+        def gather_words(a, j0, j1, tag=""):
+            tile = sb("got_w%d_%d" % (a, j0), [P, j1 - j0], U32, tag=tag)
+            nc.vector.tensor_copy(tile[:], tab_w[a][:].bitcast(U32).indirect(listed(j0, j1)))
+            for j in range(j0, j1, NARROW):
+                got_w[a, j] = (tile, j0)
 
         def up_pass(out, a, t, j0, j1, start, stop):
+            tile, base = got_w[a, j0]
             nc.tensor.matmul_mx(
                 out=out,
                 lhsT=wu_q[a][:, t * P : (t + 1) * P].bitcast(FP8X4),
                 lhsT_scale=wu_s[a][:, t * P : (t + 1) * P],
-                rhs=got_w[a][:, j0:j1].bitcast(FP8X4),
+                rhs=tile[:, j0 - base : j1 - base].bitcast(FP8X4),
                 rhs_scale=got_sc[4 * a : P, j0:j1],
                 start=start, stop=stop,
             )
 
+        gather_words(0, 0, J)
         nc.vector.tensor_copy(got_sc[:], tab_sc[:].indirect(offsets[:]))
-        round_wu(0)
-        gather_words(0, 0, J // 2)
-        quantise_wu(0)
-        gather_words(0, J // 2, J)
+        for a in range(2):
+            round_wu(2 * a)
+            round_wu(2 * a + 1)
+            quantise_wu(a)
         half = J // 2
-        narrow = [psum.tile([P, PACK, NARROW], F32, name="narrow%d" % c, tag="bank") for c in range(half // NARROW)]
-        wide = [psum.tile([P, BANK], F32, name="wide%d" % t, tag="bank") for t in range(PACK)]
-        for c in range(half // NARROW):
+        quarter = J // 4
+        def bank_tile(name, shape, bank):
+            return psum.tile(shape, F32, name=name, tag="bank%d" % bank)
+
+        narrow = [bank_tile("narrow%d" % c, [P, PACK, NARROW], c) for c in range(half // NARROW)]
+
+        def up_narrow(a, c):
             for t in range(PACK):
-                up_pass(narrow[c][:, t, :], 0, t, c * NARROW, (c + 1) * NARROW, t == 0, False)
-        for t in range(PACK):
-            up_pass(wide[t][:], 0, t, half, J, True, False)
-        round_wu(1)
-        round_wu(2)
-        quantise_wu(1)
+                up_pass(
+                    narrow[c][:, t, :], a, t, c * NARROW, (c + 1) * NARROW,
+                    a == 0 and t == 0, a == 1 and t == PACK - 1,
+                )
+
+        for c in range(len(narrow)):
+            up_narrow(0, c)
 
         h_q = [sb("h_q%d" % u, [P, half], U32) for u in range(2)]
         h_s = [sb("h_s%d" % u, [P, half], U8) for u in range(2)]
-        act = [sb("act%d" % c, [P, NARROW, PACK], F32) for c in range(half // NARROW)]
-        h_bf = [sb("h_bf%d" % c, [P, NARROW, PACK], BF16) for c in range(half // NARROW)]
 
-        def hidden_narrow(c):
-            j0, j1 = c * NARROW, (c + 1) * NARROW
-            for t in range(PACK):
-                up_pass(narrow[c][:, t, :], 1, t, j0, j1, False, t == PACK - 1)
-            nc.scalar.activation(act[c][:], narrow[c][:].rearrange("p t j -> p j t"), ACT.Silu)
-            nc.vector.tensor_tensor(
-                h_bf[c][:], act[c][:], sm_sb[:].unsqueeze(1).to_broadcast([P, NARROW, PACK]), MULT
-            )
+        def quantise_hidden(j0, j1, h_bf):
+            u = j0 // half
+            cols = slice(j0 - u * half, j1 - u * half)
             nc.vector.quantize_mx(
-                out=h_q[0][:, j0:j1].bitcast(FP8X4), scales=h_s[0][:, j0:j1],
-                in_=h_bf[c][:].rearrange("p j t -> p (j t)"),
+                out=h_q[u][:, cols].bitcast(FP8X4), scales=h_s[u][:, cols],
+                in_=h_bf[:].rearrange("p j t -> p (j t)"),
             )
+
+        def hidden_narrow(j0, j1):
+            h_bf = sb("h_bf%d" % j0, [P, j1 - j0, PACK], BF16)
+            for c in range(j0 // NARROW, j1 // NARROW):
+                up_narrow(1, c)
+                act = sb("act%d" % c, [P, NARROW, PACK], F32)
+                nc.scalar.activation(act[:], narrow[c][:].rearrange("p t j -> p j t"), ACT.Silu)
+                nc.vector.tensor_tensor(
+                    h_bf[:, c * NARROW - j0 : (c + 1) * NARROW - j0, :], act[:],
+                    sm_sb[:].unsqueeze(1).to_broadcast([P, NARROW, PACK]), MULT,
+                )
+            quantise_hidden(j0, j1, h_bf)
+
+        def hidden_wide(j0, j1):
+            width = j1 - j0
+            act = sb("act_planes", [P, PACK, width], F32)
+            planes = sb("h_planes", [P, PACK, width], BF16)
+            h_bf = sb("h_bf%d" % j0, [P, width, PACK], BF16)
+            for t in range(PACK):
+                bank = bank_tile("wide%d" % t, [P, width], t)
+                for a in range(2):
+                    up_pass(bank[:], a, t, j0, j1, a == 0, a == 1)
+                nc.scalar.activation(act[:, t, :], bank[:], ACT.Silu)
+                nc.scalar.activation(planes[:, t, :], act[:, t, :], ACT.Copy, scale=sm_sb[:, t : t + 1])
+            nc.scalar.copy(
+                out=h_bf[:].rearrange("p (c i) t -> p c t i", i=4),
+                in_=planes[:].rearrange("p t (c i) -> p c t i", i=4),
+            )
+            quantise_hidden(j0, j1, h_bf)
 
         wd8 = sb("wd8", [P, N], I32)
         wd4 = sb("wd4", [P, 2 * N], U8)
-        wd_sc = sb("wd_sc", [P, N], U8)
+        wd_sc = sb("wd_sc", [P, 2 * N], U8)
 
         def deal_wd():
             nc.vector.tensor_copy(
                 wd8[:].rearrange("p (t m) -> p m t", t=PACK), wd8_raw[:].rearrange("p (m t) -> p m t", t=PACK)
             )
             nc.vector.tensor_copy(
-                wd4[:].rearrange("p (t m e) -> p m t e", t=PACK, e=2),
-                wd4_raw[:].rearrange("p (m t e) -> p m t e", t=PACK, e=2),
+                wd4[:].bitcast(U16).rearrange("p (t m) -> p m t", t=PACK),
+                wd4_raw[:].bitcast(U16).rearrange("p (m t) -> p m t", t=PACK),
             )
             nc.vector.tensor_copy(
-                wd_sc[:].rearrange("p (t m) -> p m t", t=PACK), wd_sc_raw[:].rearrange("p (m t) -> p m t", t=PACK)
+                wd_sc[:].rearrange("p (w t m) -> p w m t", w=2, t=PACK),
+                wd_sc_raw[:].rearrange("p (w m t) -> p w m t", w=2, t=PACK),
             )
 
-        def down(t, j0, j1, y_out):
+        def down(t, j0, j1, bank_index):
             u = j0 // half
             width = j1 - j0
             step = BANK if width == BANK else NARROW
-            bank = psum.tile([P, width], F32, name="down", tag="bank")
+            bank = bank_tile("down", [P, width], bank_index)
             for c0 in range(0, width, step):
                 cols = slice(j0 - u * half + c0, j0 - u * half + c0 + step)
                 nc.tensor.matmul_mx(
@@ -205,64 +234,51 @@ def tile_list_modp_silu_res_resbP_kernel(
                 nc.tensor.matmul_mx(
                     out=bank[:, c0 : c0 + step],
                     lhsT=wd8[:, t * P : (t + 1) * P].bitcast(FP8X4),
-                    lhsT_scale=wd_sc[4:P, t * P : (t + 1) * P],
+                    lhsT_scale=wd_sc[:, N + t * P : N + (t + 1) * P],
                     rhs=h_q[u][:, cols].bitcast(FP8X4), rhs_scale=h_s[u][:, cols],
                     start=False, stop=True,
                 )
-            nc.scalar.activation(y_out, bank[:], ACT.Identity, bias=b_sb[:, t : t + 1])
-
-        quarter = J // 4
-        gather_words(1, 0, quarter)
-        deal_wd()
-        hidden_narrow(0)
-        hidden_narrow(1)
-        gather_words(1, quarter, half)
-        gather_words(1, half, J)
+            nc.scalar.activation(y_view(t, j0, j1), bank[:], ACT.Identity, bias=b_sb[:, t : t + 1])
 
         first, second, third, last = SLICE_ORDER
-        y_sb = {t: sb("y_sb%d" % t, [P, J], F32) for t in SLICE_ORDER}
-        for t in (first, second):
-            down(t, 0, quarter, y_sb[t][:, 0:quarter])
-        hidden_narrow(2)
-        hidden_narrow(3)
-        for t in (first, second):
-            down(t, quarter, half, y_sb[t][:, quarter:half])
-
-        act_wide = sb("act_wide", [P, PACK, half], F32)
-        h_planes = sb("h_planes", [P, PACK, half], BF16)
-        h_wide = sb("h_wide", [P, half, PACK], BF16)
-        for t in range(PACK):
-            up_pass(wide[t][:], 1, t, half, J, False, True)
-            nc.scalar.activation(act_wide[:, t, :], wide[t][:], ACT.Silu)
-            nc.scalar.activation(h_planes[:, t, :], act_wide[:, t, :], ACT.Copy, scale=sm_sb[:, t : t + 1])
-        nc.scalar.copy(
-            out=h_wide[:].rearrange("p (c i) t -> p c t i", i=4),
-            in_=h_planes[:].rearrange("p t (c i) -> p c t i", i=4),
-        )
-        nc.vector.quantize_mx(
-            out=h_q[1][:].bitcast(FP8X4), scales=h_s[1][:], in_=h_wide[:].rearrange("p j t -> p (j t)")
-        )
-        for t in (first, second):
-            down(t, half, J, y_sb[t][:, half:J])
-        for t in (third, last):
-            down(t, 0, half, y_sb[t][:, 0:half])
-            down(t, half, J, y_sb[t][:, half:J])
-
-        out_rows = out_0.rearrange("(p t) c -> p t c", t=PACK)
-        woven = [sb("woven%d" % g, [P, BLOCK, PACK], BF16) for g in range(T // BLOCK)]
-        ring = sb("ring", [P, 2, J], F32)
         units = [(t, j0, j1) for j0, j1 in ((0, quarter), (quarter, half), (half, J)) for t in (first, second)]
         units = units + [(third, 0, J), (last, 0, J)]
+        y_sb = {(t, j0): sb("y_sb%d_%d" % (t, j0), [P, j1 - j0], F32) for t, j0, j1 in units}
 
+        def y_view(t, j0, j1):
+            base = j0 if (t, j0) in y_sb else 0
+            return y_sb[t, base][:, j0 - base : j1 - base]
+
+        deal_wd()
+        gather_words(1, 0, quarter)
+        gather_words(1, quarter, half)
+        gather_words(1, half, J)
+        for k, (j0, j1) in enumerate(((0, quarter), (quarter, half))):
+            hidden_narrow(j0, j1)
+            down(first, j0, j1, 4 + 2 * k)
+            down(second, j0, j1, 5 + 2 * k)
+        hidden_wide(half, J)
+        down(first, half, J, 4)
+        down(second, half, J, 5)
+        down(third, 0, half, 6)
+        down(third, half, J, 0)
+        down(last, 0, half, 7)
+        down(last, half, J, 1)
+
+        out_rows = out_0.rearrange("(p t) c -> p t c", t=PACK)
+        woven = [sb("woven%d" % g, [P, c1 - c0, PACK], BF16) for g, (c0, c1) in enumerate(BLOCKS)]
+        ring = sb("ring", [P, 3, J], F32)
         sums = {}
 
         def add_residual(k):
             t, j0, j1 = units[k]
             if t == last:
                 sums[k] = sb("last_sum", [P, J], F32, tag="page%d" % first)[:]
+            elif (t, j1) == (second, half):
+                sums[k] = sb("late_sum", [P, quarter], F32, tag="h_bf%d" % half)[:]
             else:
-                sums[k] = ring[:, k % 2, 0 : j1 - j0]
-            nc.vector.tensor_tensor(sums[k], res[t][:].indirect(listed(j0, j1)), y_sb[t][:, j0:j1], ADD)
+                sums[k] = ring[:, k % 3, 0 : j1 - j0]
+            nc.vector.tensor_tensor(sums[k], res[t][:].indirect(listed(j0, j1)), y_view(t, j0, j1), ADD)
 
         def scatter(k):
             t, j0, j1 = units[k]
@@ -272,34 +288,40 @@ def tile_list_modp_silu_res_resbP_kernel(
             if j1 == J:
                 nc.sync.dma_start(out=out_rows[:, t, :], in_=page[t][:])
                 if t != last:
-                    for g in range(T // BLOCK):
-                        nc.scalar.copy(out=woven[g][:, :, t], in_=page[t][:, g * BLOCK : (g + 1) * BLOCK])
+                    for g, (c0, c1) in enumerate(BLOCKS):
+                        nc.scalar.copy(out=woven[g][:, :, t], in_=page[t][:, c0:c1])
 
         add_residual(0)
+        for t, dead in ((third, "h_bf%d" % quarter), (last, "y_sb%d_0" % first)):
+            page[t] = sb("page%d" % t, [P, T], F32, tag=dead)
+            nc.gpsimd.memset(page[t][:], 0.0)
         for k in range(len(units)):
             if k + 1 < len(units):
                 add_residual(k + 1)
             scatter(k)
 
-        out_q = [sb("out_q%d" % g, [P, BLOCK], I32) for g in range(T // BLOCK)]
+        out_q = [sb("out_q%d" % c0, [P, c1 - c0], I32) for c0, c1 in STORES]
         out_s = sb("out_s", [P, T], U8)
         words_out = out_1[0].rearrange("p t i -> p (t i)").bitcast(I32)
 
         def weave_last(g):
-            c0 = g * BLOCK
-            nc.vector.tensor_copy(woven[g][:, 0:VECTOR_SHARE, last], page[last][:, c0 : c0 + VECTOR_SHARE])
-            nc.scalar.copy(out=woven[g][:, VECTOR_SHARE:BLOCK, last], in_=page[last][:, c0 + VECTOR_SHARE : c0 + BLOCK])
+            c0, c1 = BLOCKS[g]
+            share = (c1 - c0) // 2
+            nc.vector.tensor_copy(woven[g][:, 0:share, last], page[last][:, c0 : c0 + share])
+            nc.scalar.copy(out=woven[g][:, share : c1 - c0, last], in_=page[last][:, c0 + share : c1])
 
         weave_last(0)
-        for g in range(T // BLOCK):
-            if g + 1 < T // BLOCK:
+        for g, (c0, c1) in enumerate(BLOCKS):
+            if g + 1 < len(BLOCKS):
                 weave_last(g + 1)
-            cols = slice(g * BLOCK, (g + 1) * BLOCK)
+            k = [s0 <= c0 < s1 for s0, s1 in STORES].index(True)
+            s0, s1 = STORES[k]
             nc.vector.quantize_mx(
-                out=out_q[g][:].bitcast(FP8X4), scales=out_s[:, cols],
+                out=out_q[k][:, c0 - s0 : c1 - s0].bitcast(FP8X4), scales=out_s[:, c0:c1],
                 in_=woven[g][:].rearrange("p c t -> p (c t)"),
             )
-            nc.sync.dma_start(out=words_out[:, cols], in_=out_q[g][:])
+            if c1 == s1:
+                nc.sync.dma_start(out=words_out[:, s0:s1], in_=out_q[k][:])
         for q in range(4):
             queue = nc.scalar if q % 2 else nc.sync
             queue.dma_start(

@@ -48,22 +48,13 @@ def tile_list_modp_silu_res_resbP_kernel(
         nc.gpsimd.memset(tab_sc[:].bitcast(I32), 0)
         wd_sc_raw = sb("wd_sc_raw", [P, 2 * N], U8)
         nc.gpsimd.memset(wd_sc_raw[:].bitcast(I32), 0)
-        warm_in = sb("warm_in", [P, 1], F32)
-        warm_out = sb("warm_out", [P, 1], F32)
-        nc.gpsimd.memset(warm_in[:], 0.0)
-        nc.scalar.activation(warm_out[:], warm_in[:], ACT.Silu)
 
         wu_rows = [wu[512 * a : 512 * (a + 1), :].rearrange("(p i) r -> p i r", i=PACK) for a in range(2)]
         tab_w = [sb("tab_w%d" % a, [P, T], I32) for a in range(2)]
-        wu_parts = [(a, r0, r0 + R // 2) for a in range(2) for r0 in (0, R // 2)]
-        wu_raw = [sb("wu_raw%d" % u, [P, PACK, r1 - r0], F32) for u, (a, r0, r1) in enumerate(wu_parts)]
+        wu_raw = [sb("wu_raw%d" % a, [P, PACK, R], F32) for a in range(2)]
 
         def load_table(a):
             nc.sync.dma_start(out=tab_w[a][:], in_=tab_words[a].rearrange("p t i -> p (t i)").bitcast(I32))
-
-        def load_wu(u):
-            a, r0, r1 = wu_parts[u]
-            nc.sync.dma_start(out=wu_raw[u][:], in_=wu_rows[a][:, :, r0:r1])
 
         load_table(0)
         for q in range(4):
@@ -71,8 +62,8 @@ def tile_list_modp_silu_res_resbP_kernel(
                 out=tab_sc[32 * q : 32 * q + 8, :].bitcast(I32),
                 in_=tab_scales[:, 4 * q : 4 * q + 4, :].bitcast(I32),
             )
-        for u in range(len(wu_parts)):
-            load_wu(u)
+        for a in range(2):
+            nc.sync.dma_start(out=wu_raw[a][:], in_=wu_rows[a])
         wd8_raw = sb("wd8_raw", [P, N], I32)
         nc.sync.dma_start(out=wd8_raw[:], in_=wd8_words[0].rearrange("p n i -> p (n i)").bitcast(I32))
         wd4_raw = sb("wd4_raw", [P, 2 * N], U8)
@@ -96,19 +87,18 @@ def tile_list_modp_silu_res_resbP_kernel(
         for t in SLICE_ORDER[1:]:
             nc.sync.dma_start(out=res[t][:], in_=res_rows[:, t, :])
 
-        page = {t: sb("page%d" % t, [P, T], F32) for t in SLICE_ORDER[:2]}
-        for t in SLICE_ORDER[:2]:
+        page = {t: sb("page%d" % t, [P, T], F32) for t in SLICE_ORDER}
+        for t in SLICE_ORDER:
             nc.vector.memset(page[t][:].bitcast(I32), 0)
 
         wu_bf = [sb("wu_bf%d" % a, [P, PACK, P, PACK], BF16) for a in range(2)]
         wu_q = [sb("wu_q%d" % a, [P, R], U32) for a in range(2)]
         wu_s = [sb("wu_s%d" % a, [P, R], U8) for a in range(2)]
 
-        def round_wu(u):
-            a, r0, r1 = wu_parts[u]
-            nc.scalar.copy(
+        def round_wu(copy, a, r0, r1):
+            copy(
                 out=wu_bf[a][:, :, r0 // PACK : r1 // PACK, :].rearrange("p t m i -> p m t i"),
-                in_=wu_raw[u][:].rearrange("p i (m t) -> p m t i", t=PACK),
+                in_=wu_raw[a][:, :, r0:r1].rearrange("p i (m t) -> p m t i", t=PACK),
             )
 
         def quantise_wu(a):
@@ -139,9 +129,10 @@ def tile_list_modp_silu_res_resbP_kernel(
 
         gather_words(0, 0, J)
         nc.vector.tensor_copy(got_sc[:], tab_sc[:].indirect(offsets[:]))
+        round_wu(nc.scalar.copy, 0, 0, R)
+        round_wu(nc.scalar.copy, 1, 0, R // 2)
+        round_wu(nc.vector.tensor_copy, 1, R // 2, R)
         for a in range(2):
-            round_wu(2 * a)
-            round_wu(2 * a + 1)
             quantise_wu(a)
         half = J // 2
         quarter = J // 4
@@ -292,9 +283,6 @@ def tile_list_modp_silu_res_resbP_kernel(
                         nc.scalar.copy(out=woven[g][:, :, t], in_=page[t][:, c0:c1])
 
         add_residual(0)
-        for t, dead in ((third, "h_bf%d" % quarter), (last, "y_sb%d_0" % first)):
-            page[t] = sb("page%d" % t, [P, T], F32, tag=dead)
-            nc.gpsimd.memset(page[t][:], 0.0)
         for k in range(len(units)):
             if k + 1 < len(units):
                 add_residual(k + 1)

@@ -21,7 +21,7 @@ P = 128
 PACK = 4
 BANK = 512
 NARROW = 128
-SLICE_ORDER = (2, 0, 1, 3)
+SLICE_ORDER = (0, 2, 1, 3)
 BLOCKS = ((0, 512), (512, 1024), (1024, 1536), (1536, 2048))
 STORES = BLOCKS
 
@@ -47,7 +47,10 @@ def tile_list_modp_silu_res_resbP_kernel(
         tab_sc = sb("tab_sc", [P, T], U8)
         nc.gpsimd.memset(tab_sc[:].bitcast(I32), 0)
         wd_sc_raw = sb("wd_sc_raw", [P, 2 * N], U8)
-        nc.gpsimd.memset(wd_sc_raw[:].bitcast(I32), 0)
+        nc.vector.memset(wd_sc_raw[:].bitcast(I32), 0)
+        warm = sb("warm", [P, 2], F32)
+        nc.vector.memset(warm[:, 0:1], 0.0)
+        nc.scalar.activation(warm[:, 1:2], warm[:, 0:1], ACT.Silu)
 
         wu_rows = [wu[512 * a : 512 * (a + 1), :].rearrange("(p i) r -> p i r", i=PACK) for a in range(2)]
         tab_w = [sb("tab_w%d" % a, [P, T], I32) for a in range(2)]
@@ -56,27 +59,30 @@ def tile_list_modp_silu_res_resbP_kernel(
         def load_table(a):
             nc.sync.dma_start(out=tab_w[a][:], in_=tab_words[a].rearrange("p t i -> p (t i)").bitcast(I32))
 
-        load_table(0)
+        wd8_raw = sb("wd8_raw", [P, N], I32)
+        nc.sync.dma_start(out=wd8_raw[:], in_=wd8_words[0].rearrange("p n i -> p (n i)").bitcast(I32))
+        wd4_raw = sb("wd4_raw", [P, 2 * N], U8)
+        nc.sync.dma_start(out=wd4_raw[:].bitcast(I32), in_=wd4_words[0].bitcast(I32))
         for q in range(4):
             nc.sync.dma_start(
                 out=tab_sc[32 * q : 32 * q + 8, :].bitcast(I32),
                 in_=tab_scales[:, 4 * q : 4 * q + 4, :].bitcast(I32),
             )
+        load_table(0)
         for a in range(2):
             nc.sync.dma_start(out=wu_raw[a][:], in_=wu_rows[a])
-        wd8_raw = sb("wd8_raw", [P, N], I32)
-        nc.sync.dma_start(out=wd8_raw[:], in_=wd8_words[0].rearrange("p n i -> p (n i)").bitcast(I32))
-        wd4_raw = sb("wd4_raw", [P, 2 * N], U8)
-        nc.sync.dma_start(out=wd4_raw[:].bitcast(I32), in_=wd4_words[0].bitcast(I32))
-        for tier, (scales, queue) in enumerate(((wd4_scales, nc.gpsimd), (wd8_scales, nc.sync))):
+        def load_wd_scales(tier, scales):
             for q in range(4):
-                queue.dma_start(
+                nc.sync.dma_start(
                     out=wd_sc_raw[32 * q : 32 * q + 4, tier * N : (tier + 1) * N].bitcast(I32),
                     in_=scales[0, 4 * q : 4 * q + 4, :].bitcast(I32),
                 )
+
+        load_wd_scales(0, wd4_scales)
         load_table(1)
+        load_wd_scales(1, wd8_scales)
         sm_sb = sb("sm_sb", [P, PACK], F32)
-        nc.sync.dma_start(out=sm_sb[:], in_=sm.rearrange("(p t) -> p t", t=PACK))
+        nc.gpsimd.dma_start(out=sm_sb[:], in_=sm.rearrange("(p t) -> p t", t=PACK))
         b_sb = sb("b_sb", [P, PACK], F32)
         nc.gpsimd.dma_start(out=b_sb[:], in_=b.rearrange("(p t) -> p t", t=PACK))
         res = {t: sb("res%d" % t, [P, T], F32) for t in SLICE_ORDER}
@@ -87,9 +93,10 @@ def tile_list_modp_silu_res_resbP_kernel(
         for t in SLICE_ORDER[1:]:
             nc.sync.dma_start(out=res[t][:], in_=res_rows[:, t, :])
 
-        page = {t: sb("page%d" % t, [P, T], F32) for t in SLICE_ORDER}
-        for t in SLICE_ORDER:
-            nc.vector.memset(page[t][:].bitcast(I32), 0)
+        page = {t: sb("page%d" % t, [P, T], F32) for t in SLICE_ORDER[:2]}
+        for k in range(2):
+            nc.vector.memset(page[SLICE_ORDER[k]][:].bitcast(I32), 0)
+            page[SLICE_ORDER[k + 2]] = page[SLICE_ORDER[k]]
 
         wu_bf = [sb("wu_bf%d" % a, [P, PACK, P, PACK], BF16) for a in range(2)]
         wu_q = [sb("wu_q%d" % a, [P, R], U32) for a in range(2)]
@@ -97,8 +104,8 @@ def tile_list_modp_silu_res_resbP_kernel(
 
         def round_wu(copy, a, r0, r1):
             copy(
-                out=wu_bf[a][:, :, r0 // PACK : r1 // PACK, :].rearrange("p t m i -> p m t i"),
-                in_=wu_raw[a][:, :, r0:r1].rearrange("p i (m t) -> p m t i", t=PACK),
+                out=wu_bf[a][:, :, r0 // PACK : r1 // PACK, :].rearrange("p t m i -> p m i t"),
+                in_=wu_raw[a][:, :, r0:r1].rearrange("p i (m t) -> p m i t", t=PACK),
             )
 
         def quantise_wu(a):
@@ -127,11 +134,11 @@ def tile_list_modp_silu_res_resbP_kernel(
                 start=start, stop=stop,
             )
 
-        gather_words(0, 0, J)
         nc.vector.tensor_copy(got_sc[:], tab_sc[:].indirect(offsets[:]))
+        gather_words(0, 0, J)
         round_wu(nc.scalar.copy, 0, 0, R)
-        round_wu(nc.scalar.copy, 1, 0, R // 2)
-        round_wu(nc.vector.tensor_copy, 1, R // 2, R)
+        round_wu(nc.scalar.copy, 1, 0, 3 * R // 4)
+        round_wu(nc.vector.tensor_copy, 1, 3 * R // 4, R)
         for a in range(2):
             quantise_wu(a)
         half = J // 2
@@ -203,10 +210,12 @@ def tile_list_modp_silu_res_resbP_kernel(
                 wd4[:].bitcast(U16).rearrange("p (t m) -> p m t", t=PACK),
                 wd4_raw[:].bitcast(U16).rearrange("p (m t) -> p m t", t=PACK),
             )
-            nc.vector.tensor_copy(
-                wd_sc[:].rearrange("p (w t m) -> p w m t", w=2, t=PACK),
-                wd_sc_raw[:].rearrange("p (w m t) -> p w m t", w=2, t=PACK),
-            )
+            for tier in range(2):
+                cols = slice(tier * N, (tier + 1) * N)
+                nc.vector.tensor_copy(
+                    wd_sc[:, cols].rearrange("p (t m) -> p m t", t=PACK),
+                    wd_sc_raw[:, cols].rearrange("p (m t) -> p m t", t=PACK),
+                )
 
         def down(t, j0, j1, bank_index):
             u = j0 // half
@@ -234,7 +243,8 @@ def tile_list_modp_silu_res_resbP_kernel(
         first, second, third, last = SLICE_ORDER
         units = [(t, j0, j1) for j0, j1 in ((0, quarter), (quarter, half), (half, J)) for t in (first, second)]
         units = units + [(third, 0, J), (last, 0, J)]
-        y_sb = {(t, j0): sb("y_sb%d_%d" % (t, j0), [P, j1 - j0], F32) for t, j0, j1 in units}
+        held = (second, quarter)
+        y_sb = {(t, j0): sb("y_sb%d_%d" % (t, j0), [P, j1 - j0], F32) for t, j0, j1 in units if (t, j0) != held}
 
         def y_view(t, j0, j1):
             base = j0 if (t, j0) in y_sb else 0
@@ -247,8 +257,11 @@ def tile_list_modp_silu_res_resbP_kernel(
         for k, (j0, j1) in enumerate(((0, quarter), (quarter, half))):
             hidden_narrow(j0, j1)
             down(first, j0, j1, 4 + 2 * k)
-            down(second, j0, j1, 5 + 2 * k)
+            if (second, j0) != held:
+                down(second, j0, j1, 5 + 2 * k)
         hidden_wide(half, J)
+        y_sb[held] = sb("y_held", [P, quarter], F32, tag="h_planes")
+        down(second, quarter, half, 7)
         down(first, half, J, 4)
         down(second, half, J, 5)
         down(third, 0, half, 6)
@@ -263,12 +276,7 @@ def tile_list_modp_silu_res_resbP_kernel(
 
         def add_residual(k):
             t, j0, j1 = units[k]
-            if t == last:
-                sums[k] = sb("last_sum", [P, J], F32, tag="page%d" % first)[:]
-            elif (t, j1) == (second, half):
-                sums[k] = sb("late_sum", [P, quarter], F32, tag="h_bf%d" % half)[:]
-            else:
-                sums[k] = ring[:, k % 3, 0 : j1 - j0]
+            sums[k] = ring[:, k % 3, 0 : j1 - j0]
             nc.vector.tensor_tensor(sums[k], res[t][:].indirect(listed(j0, j1)), y_view(t, j0, j1), ADD)
 
         def scatter(k):

@@ -22,7 +22,7 @@ PACK = 4
 BANK = 512
 NARROW = 128
 SLICE_ORDER = (0, 2, 1, 3)
-BLOCKS = ((0, 512), (512, 1024), (1024, 1536), (1536, 2048))
+BLOCKS = ((0, 512), (512, 1024), (1024, 1536), (1536, 1792), (1792, 2048))
 STORES = BLOCKS
 
 
@@ -71,32 +71,38 @@ def tile_list_modp_silu_res_resbP_kernel(
         load_table(0)
         for a in range(2):
             nc.sync.dma_start(out=wu_raw[a][:], in_=wu_rows[a])
-        def load_wd_scales(tier, scales):
+        def load_wd_scales(queue, tier, scales):
             for q in range(4):
-                nc.sync.dma_start(
+                queue.dma_start(
                     out=wd_sc_raw[32 * q : 32 * q + 4, tier * N : (tier + 1) * N].bitcast(I32),
                     in_=scales[0, 4 * q : 4 * q + 4, :].bitcast(I32),
                 )
 
-        load_wd_scales(0, wd4_scales)
+        load_wd_scales(nc.gpsimd, 0, wd4_scales)
+        load_wd_scales(nc.sync, 1, wd8_scales)
         load_table(1)
-        load_wd_scales(1, wd8_scales)
         sm_sb = sb("sm_sb", [P, PACK], F32)
-        nc.gpsimd.dma_start(out=sm_sb[:], in_=sm.rearrange("(p t) -> p t", t=PACK))
+        nc.sync.dma_start(out=sm_sb[:], in_=sm.rearrange("(p t) -> p t", t=PACK))
         b_sb = sb("b_sb", [P, PACK], F32)
-        nc.gpsimd.dma_start(out=b_sb[:], in_=b.rearrange("(p t) -> p t", t=PACK))
+        nc.sync.dma_start(out=b_sb[:], in_=b.rearrange("(p t) -> p t", t=PACK))
         res = {t: sb("res%d" % t, [P, T], F32) for t in SLICE_ORDER}
         res_rows = rT.rearrange("(p t) c -> p t c", t=PACK)
         nc.sync.dma_start(out=res[SLICE_ORDER[0]][:], in_=res_rows[:, SLICE_ORDER[0], :])
+        nc.sync.dma_start(out=res[SLICE_ORDER[1]][:], in_=res_rows[:, SLICE_ORDER[1], :])
         wgo_sb = sb("wgo_sb", [P, J], F32)
         nc.sync.dma_start(out=wgo_sb[:], in_=wgo)
-        for t in SLICE_ORDER[1:]:
+        for t in SLICE_ORDER[2:]:
             nc.sync.dma_start(out=res[t][:], in_=res_rows[:, t, :])
 
-        page = {t: sb("page%d" % t, [P, T], F32) for t in SLICE_ORDER[:2]}
-        for k in range(2):
-            nc.vector.memset(page[SLICE_ORDER[k]][:].bitcast(I32), 0)
-            page[SLICE_ORDER[k + 2]] = page[SLICE_ORDER[k]]
+        page = {}
+
+        def clear_page(engine, k, tag=""):
+            tile = sb("page%d" % k, [P, T], F32, tag=tag)
+            engine.memset(tile[:].bitcast(I32), 0)
+            page[SLICE_ORDER[k]] = tile
+            page[SLICE_ORDER[k + 2]] = tile
+
+        clear_page(nc.vector, 0)
 
         wu_bf = [sb("wu_bf%d" % a, [P, PACK, P, PACK], BF16) for a in range(2)]
         wu_q = [sb("wu_q%d" % a, [P, R], U32) for a in range(2)]
@@ -137,8 +143,8 @@ def tile_list_modp_silu_res_resbP_kernel(
         nc.vector.tensor_copy(got_sc[:], tab_sc[:].indirect(offsets[:]))
         gather_words(0, 0, J)
         round_wu(nc.scalar.copy, 0, 0, R)
-        round_wu(nc.scalar.copy, 1, 0, 3 * R // 4)
-        round_wu(nc.vector.tensor_copy, 1, 3 * R // 4, R)
+        round_wu(nc.scalar.copy, 1, 0, R // 2)
+        round_wu(nc.vector.tensor_copy, 1, R // 2, R)
         for a in range(2):
             quantise_wu(a)
         half = J // 2
@@ -170,7 +176,7 @@ def tile_list_modp_silu_res_resbP_kernel(
             )
 
         def hidden_narrow(j0, j1):
-            h_bf = sb("h_bf%d" % j0, [P, j1 - j0, PACK], BF16)
+            h_bf = sb("h_bf%d" % j0, [P, j1 - j0, PACK], BF16, )
             for c in range(j0 // NARROW, j1 // NARROW):
                 up_narrow(1, c)
                 act = sb("act%d" % c, [P, NARROW, PACK], F32)
@@ -179,6 +185,8 @@ def tile_list_modp_silu_res_resbP_kernel(
                     h_bf[:, c * NARROW - j0 : (c + 1) * NARROW - j0, :], act[:],
                     sm_sb[:].unsqueeze(1).to_broadcast([P, NARROW, PACK]), MULT,
                 )
+            if j0 == 0:
+                deal_scales(0, "act0")
             quantise_hidden(j0, j1, h_bf)
 
         def hidden_wide(j0, j1):
@@ -200,7 +208,14 @@ def tile_list_modp_silu_res_resbP_kernel(
 
         wd8 = sb("wd8", [P, N], I32)
         wd4 = sb("wd4", [P, 2 * N], U8)
-        wd_sc = sb("wd_sc", [P, 2 * N], U8)
+        wd_sc = {}
+
+        def deal_scales(tier, tag=""):
+            wd_sc[tier] = sb("wd_sc%d" % tier, [P, N], U8, tag=tag)
+            nc.vector.tensor_copy(
+                wd_sc[tier][:].rearrange("p (t m) -> p m t", t=PACK),
+                wd_sc_raw[:, tier * N : (tier + 1) * N].rearrange("p (m t) -> p m t", t=PACK),
+            )
 
         def deal_wd():
             nc.vector.tensor_copy(
@@ -210,12 +225,7 @@ def tile_list_modp_silu_res_resbP_kernel(
                 wd4[:].bitcast(U16).rearrange("p (t m) -> p m t", t=PACK),
                 wd4_raw[:].bitcast(U16).rearrange("p (m t) -> p m t", t=PACK),
             )
-            for tier in range(2):
-                cols = slice(tier * N, (tier + 1) * N)
-                nc.vector.tensor_copy(
-                    wd_sc[:, cols].rearrange("p (t m) -> p m t", t=PACK),
-                    wd_sc_raw[:, cols].rearrange("p (m t) -> p m t", t=PACK),
-                )
+            deal_scales(1)
 
         def down(t, j0, j1, bank_index):
             u = j0 // half
@@ -227,14 +237,14 @@ def tile_list_modp_silu_res_resbP_kernel(
                 nc.tensor.matmul_mx(
                     out=bank[:, c0 : c0 + step],
                     lhsT=wd4[:, 2 * t * P : 2 * (t + 1) * P].bitcast(FP4X4),
-                    lhsT_scale=wd_sc[:, t * P : (t + 1) * P],
+                    lhsT_scale=wd_sc[0][:, t * P : (t + 1) * P],
                     rhs=h_q[u][:, cols].bitcast(FP8X4), rhs_scale=h_s[u][:, cols],
                     start=True, stop=False,
                 )
                 nc.tensor.matmul_mx(
                     out=bank[:, c0 : c0 + step],
                     lhsT=wd8[:, t * P : (t + 1) * P].bitcast(FP8X4),
-                    lhsT_scale=wd_sc[:, N + t * P : N + (t + 1) * P],
+                    lhsT_scale=wd_sc[1][:, t * P : (t + 1) * P],
                     rhs=h_q[u][:, cols].bitcast(FP8X4), rhs_scale=h_s[u][:, cols],
                     start=False, stop=True,
                 )
@@ -251,6 +261,7 @@ def tile_list_modp_silu_res_resbP_kernel(
             return y_sb[t, base][:, j0 - base : j1 - base]
 
         deal_wd()
+        clear_page(nc.gpsimd, 1, "wd8_raw")
         gather_words(1, 0, quarter)
         gather_words(1, quarter, half)
         gather_words(1, half, J)

@@ -20,10 +20,12 @@ MULT = mybir.AluOpType.mult
 P = 128
 PACK = 4
 BANK = 512
-NARROW = 128
+NARROW = BANK // PACK
+HALF = J // 2
+QUARTER = J // 4
+SUMS_IN_FLIGHT = 3
 SLICE_ORDER = (0, 2, 1, 3)
 BLOCKS = ((0, 512), (512, 1024), (1024, 1536), (1536, 1792), (1792, 2048))
-STORES = BLOCKS
 
 
 def tile_list_modp_silu_res_resbP_kernel(
@@ -31,12 +33,16 @@ def tile_list_modp_silu_res_resbP_kernel(
     out_0, out_1, out_2,
 ):
     nc = tc.nc
+    first, second, third, last = SLICE_ORDER
     with ExitStack() as ctx:
         keep = ctx.enter_context(tc.tile_pool(name="keep", bufs=1))
         psum = ctx.enter_context(tc.psum_pool(name="psum", bufs=1))
 
         def sb(name, shape, dtype, tag=""):
             return keep.tile(shape, dtype, name=name, tag=tag or name, align_bytes=64)
+
+        def bank_tile(name, shape, bank):
+            return psum.tile(shape, F32, name=name, tag="bank%d" % bank)
 
         offsets = keep.tile([P, J // 16], U16, name="offsets")
         nc.sync.dma_start(offsets[:], offs)
@@ -48,19 +54,20 @@ def tile_list_modp_silu_res_resbP_kernel(
         nc.gpsimd.memset(tab_sc[:].bitcast(I32), 0)
         wd_sc_raw = sb("wd_sc_raw", [P, 2 * N], U8)
         nc.vector.memset(wd_sc_raw[:].bitcast(I32), 0)
-        warm = sb("warm", [P, 2], F32)
-        nc.vector.memset(warm[:, 0:1], 0.0)
-        nc.scalar.activation(warm[:, 1:2], warm[:, 0:1], ACT.Silu)
 
-        wu_rows = [wu[512 * a : 512 * (a + 1), :].rearrange("(p i) r -> p i r", i=PACK) for a in range(2)]
         tab_w = [sb("tab_w%d" % a, [P, T], I32) for a in range(2)]
         wu_raw = [sb("wu_raw%d" % a, [P, PACK, R], F32) for a in range(2)]
 
         def load_table(a):
             nc.sync.dma_start(out=tab_w[a][:], in_=tab_words[a].rearrange("p t i -> p (t i)").bitcast(I32))
 
-        wd8_raw = sb("wd8_raw", [P, N], I32)
-        nc.sync.dma_start(out=wd8_raw[:], in_=wd8_words[0].rearrange("p n i -> p (n i)").bitcast(I32))
+        def load_wd_scales(queue, tier, scales):
+            for q in range(4):
+                queue.dma_start(
+                    out=wd_sc_raw[32 * q : 32 * q + 4, tier * N : (tier + 1) * N].bitcast(I32),
+                    in_=scales[0, 4 * q : 4 * q + 4, :].bitcast(I32),
+                )
+
         wd4_raw = sb("wd4_raw", [P, 2 * N], U8)
         nc.sync.dma_start(out=wd4_raw[:].bitcast(I32), in_=wd4_words[0].bitcast(I32))
         for q in range(4):
@@ -70,39 +77,35 @@ def tile_list_modp_silu_res_resbP_kernel(
             )
         load_table(0)
         for a in range(2):
-            nc.sync.dma_start(out=wu_raw[a][:], in_=wu_rows[a])
-        def load_wd_scales(queue, tier, scales):
-            for q in range(4):
-                queue.dma_start(
-                    out=wd_sc_raw[32 * q : 32 * q + 4, tier * N : (tier + 1) * N].bitcast(I32),
-                    in_=scales[0, 4 * q : 4 * q + 4, :].bitcast(I32),
-                )
-
+            rows = wu[512 * a : 512 * (a + 1), :].rearrange("(p i) r -> p i r", i=PACK)
+            nc.sync.dma_start(out=wu_raw[a][:], in_=rows)
         load_wd_scales(nc.gpsimd, 0, wd4_scales)
         load_wd_scales(nc.sync, 1, wd8_scales)
         load_table(1)
+        wd8_raw = sb("wd8_raw", [P, N], I32)
+        nc.sync.dma_start(out=wd8_raw[:], in_=wd8_words[0].rearrange("p n i -> p (n i)").bitcast(I32))
         sm_sb = sb("sm_sb", [P, PACK], F32)
         nc.sync.dma_start(out=sm_sb[:], in_=sm.rearrange("(p t) -> p t", t=PACK))
         b_sb = sb("b_sb", [P, PACK], F32)
         nc.sync.dma_start(out=b_sb[:], in_=b.rearrange("(p t) -> p t", t=PACK))
         res = {t: sb("res%d" % t, [P, T], F32) for t in SLICE_ORDER}
         res_rows = rT.rearrange("(p t) c -> p t c", t=PACK)
-        nc.sync.dma_start(out=res[SLICE_ORDER[0]][:], in_=res_rows[:, SLICE_ORDER[0], :])
-        nc.sync.dma_start(out=res[SLICE_ORDER[1]][:], in_=res_rows[:, SLICE_ORDER[1], :])
+        for t in (first, second):
+            nc.sync.dma_start(out=res[t][:], in_=res_rows[:, t, :])
         wgo_sb = sb("wgo_sb", [P, J], F32)
         nc.sync.dma_start(out=wgo_sb[:], in_=wgo)
-        for t in SLICE_ORDER[2:]:
+        for t in (third, last):
             nc.sync.dma_start(out=res[t][:], in_=res_rows[:, t, :])
 
         page = {}
 
-        def clear_page(engine, k, tag=""):
-            tile = sb("page%d" % k, [P, T], F32, tag=tag)
+        def clear_page(engine, early, late, tag=""):
+            tile = sb("page%d" % early, [P, T], F32, tag=tag)
             engine.memset(tile[:].bitcast(I32), 0)
-            page[SLICE_ORDER[k]] = tile
-            page[SLICE_ORDER[k + 2]] = tile
+            page[early] = tile
+            page[late] = tile
 
-        clear_page(nc.vector, 0)
+        clear_page(nc.vector, first, third)
 
         wu_bf = [sb("wu_bf%d" % a, [P, PACK, P, PACK], BF16) for a in range(2)]
         wu_q = [sb("wu_q%d" % a, [P, R], U32) for a in range(2)]
@@ -114,17 +117,11 @@ def tile_list_modp_silu_res_resbP_kernel(
                 in_=wu_raw[a][:, :, r0:r1].rearrange("p i (m t) -> p m i t", t=PACK),
             )
 
-        def quantise_wu(a):
-            nc.vector.quantize_mx(
-                out=wu_q[a][:].bitcast(FP8X4), scales=wu_s[a][:],
-                in_=wu_bf[a][:].rearrange("p t m i -> p (t m i)"),
-            )
-
         got_sc = sb("got_sc", [P, J], U8)
         got_w = {}
 
-        def gather_words(a, j0, j1, tag=""):
-            tile = sb("got_w%d_%d" % (a, j0), [P, j1 - j0], U32, tag=tag)
+        def gather_words(a, j0, j1):
+            tile = sb("got_w%d_%d" % (a, j0), [P, j1 - j0], U32)
             nc.vector.tensor_copy(tile[:], tab_w[a][:].bitcast(U32).indirect(listed(j0, j1)))
             for j in range(j0, j1, NARROW):
                 got_w[a, j] = (tile, j0)
@@ -142,17 +139,15 @@ def tile_list_modp_silu_res_resbP_kernel(
 
         nc.vector.tensor_copy(got_sc[:], tab_sc[:].indirect(offsets[:]))
         gather_words(0, 0, J)
-        round_wu(nc.scalar.copy, 0, 0, R)
-        round_wu(nc.scalar.copy, 1, 0, R // 2)
-        round_wu(nc.vector.tensor_copy, 1, R // 2, R)
         for a in range(2):
-            quantise_wu(a)
-        half = J // 2
-        quarter = J // 4
-        def bank_tile(name, shape, bank):
-            return psum.tile(shape, F32, name=name, tag="bank%d" % bank)
+            round_wu(nc.scalar.copy, a, 0, R // 2)
+            round_wu(nc.vector.tensor_copy, a, R // 2, R)
+            nc.vector.quantize_mx(
+                out=wu_q[a][:].bitcast(FP8X4), scales=wu_s[a][:],
+                in_=wu_bf[a][:].rearrange("p t m i -> p (t m i)"),
+            )
 
-        narrow = [bank_tile("narrow%d" % c, [P, PACK, NARROW], c) for c in range(half // NARROW)]
+        narrow = [bank_tile("narrow%d" % c, [P, PACK, NARROW], c) for c in range(HALF // NARROW)]
 
         def up_narrow(a, c):
             for t in range(PACK):
@@ -164,19 +159,19 @@ def tile_list_modp_silu_res_resbP_kernel(
         for c in range(len(narrow)):
             up_narrow(0, c)
 
-        h_q = [sb("h_q%d" % u, [P, half], U32) for u in range(2)]
-        h_s = [sb("h_s%d" % u, [P, half], U8) for u in range(2)]
+        h_q = [sb("h_q%d" % u, [P, HALF], U32) for u in range(2)]
+        h_s = [sb("h_s%d" % u, [P, HALF], U8) for u in range(2)]
 
         def quantise_hidden(j0, j1, h_bf):
-            u = j0 // half
-            cols = slice(j0 - u * half, j1 - u * half)
+            u = j0 // HALF
+            cols = slice(j0 - u * HALF, j1 - u * HALF)
             nc.vector.quantize_mx(
                 out=h_q[u][:, cols].bitcast(FP8X4), scales=h_s[u][:, cols],
                 in_=h_bf[:].rearrange("p j t -> p (j t)"),
             )
 
         def hidden_narrow(j0, j1):
-            h_bf = sb("h_bf%d" % j0, [P, j1 - j0, PACK], BF16, )
+            h_bf = sb("h_bf%d" % j0, [P, j1 - j0, PACK], BF16)
             for c in range(j0 // NARROW, j1 // NARROW):
                 up_narrow(1, c)
                 act = sb("act%d" % c, [P, NARROW, PACK], F32)
@@ -185,55 +180,55 @@ def tile_list_modp_silu_res_resbP_kernel(
                     h_bf[:, c * NARROW - j0 : (c + 1) * NARROW - j0, :], act[:],
                     sm_sb[:].unsqueeze(1).to_broadcast([P, NARROW, PACK]), MULT,
                 )
-            if j0 == 0:
-                deal_scales(0, "act0")
-            quantise_hidden(j0, j1, h_bf)
+            return h_bf
 
         def hidden_wide(j0, j1):
             width = j1 - j0
-            act = sb("act_planes", [P, PACK, width], F32)
-            planes = sb("h_planes", [P, PACK, width], BF16)
+            act = sb("act_slices", [P, PACK, width], F32)
+            h_slices = sb("h_slices", [P, PACK, width], BF16)
             h_bf = sb("h_bf%d" % j0, [P, width, PACK], BF16)
             for t in range(PACK):
                 bank = bank_tile("wide%d" % t, [P, width], t)
                 for a in range(2):
                     up_pass(bank[:], a, t, j0, j1, a == 0, a == 1)
                 nc.scalar.activation(act[:, t, :], bank[:], ACT.Silu)
-                nc.scalar.activation(planes[:, t, :], act[:, t, :], ACT.Copy, scale=sm_sb[:, t : t + 1])
+                nc.scalar.activation(h_slices[:, t, :], act[:, t, :], ACT.Copy, scale=sm_sb[:, t : t + 1])
             nc.scalar.copy(
                 out=h_bf[:].rearrange("p (c i) t -> p c t i", i=4),
-                in_=planes[:].rearrange("p t (c i) -> p c t i", i=4),
+                in_=h_slices[:].rearrange("p t (c i) -> p c t i", i=4),
             )
-            quantise_hidden(j0, j1, h_bf)
+            return h_bf
 
         wd8 = sb("wd8", [P, N], I32)
         wd4 = sb("wd4", [P, 2 * N], U8)
         wd_sc = {}
 
+        def deal(out, in_):
+            nc.vector.tensor_copy(
+                out.rearrange("p (t m) -> p m t", t=PACK), in_.rearrange("p (m t) -> p m t", t=PACK)
+            )
+
         def deal_scales(tier, tag=""):
             wd_sc[tier] = sb("wd_sc%d" % tier, [P, N], U8, tag=tag)
-            nc.vector.tensor_copy(
-                wd_sc[tier][:].rearrange("p (t m) -> p m t", t=PACK),
-                wd_sc_raw[:, tier * N : (tier + 1) * N].rearrange("p (m t) -> p m t", t=PACK),
-            )
+            deal(wd_sc[tier][:], wd_sc_raw[:, tier * N : (tier + 1) * N])
 
-        def deal_wd():
-            nc.vector.tensor_copy(
-                wd8[:].rearrange("p (t m) -> p m t", t=PACK), wd8_raw[:].rearrange("p (m t) -> p m t", t=PACK)
-            )
-            nc.vector.tensor_copy(
-                wd4[:].bitcast(U16).rearrange("p (t m) -> p m t", t=PACK),
-                wd4_raw[:].bitcast(U16).rearrange("p (m t) -> p m t", t=PACK),
-            )
-            deal_scales(1)
+        pieces = ((0, QUARTER), (QUARTER, HALF), (HALF, J))
+        units = [(t, j0, j1) for j0, j1 in pieces for t in (first, second)]
+        units = units + [(third, 0, J), (last, 0, J)]
+        held = (second, QUARTER)
+        y_sb = {(t, j0): sb("y_sb%d_%d" % (t, j0), [P, j1 - j0], F32) for t, j0, j1 in units if (t, j0) != held}
+
+        def y_view(t, j0, j1):
+            base = j0 if (t, j0) in y_sb else 0
+            return y_sb[t, base][:, j0 - base : j1 - base]
 
         def down(t, j0, j1, bank_index):
-            u = j0 // half
+            u = j0 // HALF
             width = j1 - j0
             step = BANK if width == BANK else NARROW
             bank = bank_tile("down", [P, width], bank_index)
             for c0 in range(0, width, step):
-                cols = slice(j0 - u * half + c0, j0 - u * half + c0 + step)
+                cols = slice(j0 - u * HALF + c0, j0 - u * HALF + c0 + step)
                 nc.tensor.matmul_mx(
                     out=bank[:, c0 : c0 + step],
                     lhsT=wd4[:, 2 * t * P : 2 * (t + 1) * P].bitcast(FP4X4),
@@ -250,51 +245,43 @@ def tile_list_modp_silu_res_resbP_kernel(
                 )
             nc.scalar.activation(y_view(t, j0, j1), bank[:], ACT.Identity, bias=b_sb[:, t : t + 1])
 
-        first, second, third, last = SLICE_ORDER
-        units = [(t, j0, j1) for j0, j1 in ((0, quarter), (quarter, half), (half, J)) for t in (first, second)]
-        units = units + [(third, 0, J), (last, 0, J)]
-        held = (second, quarter)
-        y_sb = {(t, j0): sb("y_sb%d_%d" % (t, j0), [P, j1 - j0], F32) for t, j0, j1 in units if (t, j0) != held}
-
-        def y_view(t, j0, j1):
-            base = j0 if (t, j0) in y_sb else 0
-            return y_sb[t, base][:, j0 - base : j1 - base]
-
-        deal_wd()
-        clear_page(nc.gpsimd, 1, "wd8_raw")
-        gather_words(1, 0, quarter)
-        gather_words(1, quarter, half)
-        gather_words(1, half, J)
-        for k, (j0, j1) in enumerate(((0, quarter), (quarter, half))):
-            hidden_narrow(j0, j1)
-            down(first, j0, j1, 4 + 2 * k)
-            if (second, j0) != held:
-                down(second, j0, j1, 5 + 2 * k)
-        hidden_wide(half, J)
-        y_sb[held] = sb("y_held", [P, quarter], F32, tag="h_planes")
-        down(second, quarter, half, 7)
-        down(first, half, J, 4)
-        down(second, half, J, 5)
-        down(third, 0, half, 6)
-        down(third, half, J, 0)
-        down(last, 0, half, 7)
-        down(last, half, J, 1)
+        deal(wd8[:], wd8_raw[:])
+        deal(wd4[:].bitcast(U16), wd4_raw[:].bitcast(U16))
+        deal_scales(1)
+        clear_page(nc.gpsimd, second, last, "wd4_raw")
+        for j0, j1 in pieces:
+            gather_words(1, j0, j1)
+        h_bf = hidden_narrow(0, QUARTER)
+        deal_scales(0, "act0")
+        quantise_hidden(0, QUARTER, h_bf)
+        down(first, 0, QUARTER, 4)
+        down(second, 0, QUARTER, 5)
+        quantise_hidden(QUARTER, HALF, hidden_narrow(QUARTER, HALF))
+        down(first, QUARTER, HALF, 6)
+        quantise_hidden(HALF, J, hidden_wide(HALF, J))
+        y_sb[held] = sb("y_held", [P, QUARTER], F32, tag="h_slices")
+        down(second, QUARTER, HALF, 7)
+        down(first, HALF, J, 4)
+        down(second, HALF, J, 5)
+        down(third, 0, HALF, 6)
+        down(third, HALF, J, 0)
+        down(last, 0, HALF, 7)
+        down(last, HALF, J, 1)
 
         out_rows = out_0.rearrange("(p t) c -> p t c", t=PACK)
         woven = [sb("woven%d" % g, [P, c1 - c0, PACK], BF16) for g, (c0, c1) in enumerate(BLOCKS)]
-        ring = sb("ring", [P, 3, J], F32)
-        sums = {}
+        ring = sb("ring", [P, SUMS_IN_FLIGHT, J], F32)
+
+        def unit_sum(k):
+            return ring[:, k % SUMS_IN_FLIGHT, 0 : units[k][2] - units[k][1]]
 
         def add_residual(k):
             t, j0, j1 = units[k]
-            sums[k] = ring[:, k % 3, 0 : j1 - j0]
-            nc.vector.tensor_tensor(sums[k], res[t][:].indirect(listed(j0, j1)), y_view(t, j0, j1), ADD)
+            nc.vector.tensor_tensor(unit_sum(k), res[t][:].indirect(listed(j0, j1)), y_view(t, j0, j1), ADD)
 
         def scatter(k):
             t, j0, j1 = units[k]
-            nc.vector.tensor_tensor(
-                page[t][:].indirect(listed(j0, j1)), sums[k], wgo_sb[:, j0:j1], MULT
-            )
+            nc.vector.tensor_tensor(page[t][:].indirect(listed(j0, j1)), unit_sum(k), wgo_sb[:, j0:j1], MULT)
             if j1 == J:
                 nc.sync.dma_start(out=out_rows[:, t, :], in_=page[t][:])
                 if t != last:
@@ -307,28 +294,25 @@ def tile_list_modp_silu_res_resbP_kernel(
                 add_residual(k + 1)
             scatter(k)
 
-        out_q = [sb("out_q%d" % c0, [P, c1 - c0], I32) for c0, c1 in STORES]
+        out_q = [sb("out_q%d" % g, [P, c1 - c0], I32) for g, (c0, c1) in enumerate(BLOCKS)]
         out_s = sb("out_s", [P, T], U8)
         words_out = out_1[0].rearrange("p t i -> p (t i)").bitcast(I32)
 
-        def weave_last(g):
+        def round_last(g):
             c0, c1 = BLOCKS[g]
             share = (c1 - c0) // 2
             nc.vector.tensor_copy(woven[g][:, 0:share, last], page[last][:, c0 : c0 + share])
             nc.scalar.copy(out=woven[g][:, share : c1 - c0, last], in_=page[last][:, c0 + share : c1])
 
-        weave_last(0)
+        round_last(0)
         for g, (c0, c1) in enumerate(BLOCKS):
             if g + 1 < len(BLOCKS):
-                weave_last(g + 1)
-            k = [s0 <= c0 < s1 for s0, s1 in STORES].index(True)
-            s0, s1 = STORES[k]
+                round_last(g + 1)
             nc.vector.quantize_mx(
-                out=out_q[k][:, c0 - s0 : c1 - s0].bitcast(FP8X4), scales=out_s[:, c0:c1],
+                out=out_q[g][:].bitcast(FP8X4), scales=out_s[:, c0:c1],
                 in_=woven[g][:].rearrange("p c t -> p (c t)"),
             )
-            if c1 == s1:
-                nc.sync.dma_start(out=words_out[:, s0:s1], in_=out_q[k][:])
+            nc.sync.dma_start(out=words_out[:, c0:c1], in_=out_q[g][:])
         for q in range(4):
             queue = nc.scalar if q % 2 else nc.sync
             queue.dma_start(

@@ -36,9 +36,12 @@ def tile_list_modp_silu_res_resbP_kernel(
     first, second, third, last = SLICE_ORDER
     with ExitStack() as ctx:
         keep = ctx.enter_context(tc.tile_pool(name="keep", bufs=1))
+        placed = ctx.enter_context(tc.tile_pool(name="placed", bufs=1))
         psum = ctx.enter_context(tc.psum_pool(name="psum", bufs=1))
 
-        def sb(name, shape, dtype, tag=""):
+        def sb(name, shape, dtype, tag="", offset=None):
+            if offset is not None:
+                return placed.tile(shape, dtype, name=name, offset=offset, align_bytes=64)
             return keep.tile(shape, dtype, name=name, tag=tag or name, align_bytes=64)
 
         def bank_tile(name, shape, bank):
@@ -56,7 +59,14 @@ def tile_list_modp_silu_res_resbP_kernel(
         nc.vector.memset(wd_sc_raw[:].bitcast(I32), 0)
 
         tab_w = [sb("tab_w%d" % a, [P, T], I32) for a in range(2)]
-        wu_raw = [sb("wu_raw%d" % a, [P, PACK, R], F32) for a in range(2)]
+        wu_raw = {}
+        wu_loads = (((0, R),), ((0, R // 2), (R // 2, R)))
+
+        def load_wu(a, r0, r1):
+            tile = sb("wu_raw%d_%d" % (a, r0), [P, PACK, r1 - r0], F32)
+            rows = wu[512 * a : 512 * (a + 1), r0:r1].rearrange("(p i) r -> p i r", i=PACK)
+            nc.sync.dma_start(out=tile[:], in_=rows)
+            wu_raw[a, r0] = tile
 
         def load_table(a):
             nc.sync.dma_start(out=tab_w[a][:], in_=tab_words[a].rearrange("p t i -> p (t i)").bitcast(I32))
@@ -76,12 +86,12 @@ def tile_list_modp_silu_res_resbP_kernel(
                 in_=tab_scales[:, 4 * q : 4 * q + 4, :].bitcast(I32),
             )
         load_table(0)
-        for a in range(2):
-            rows = wu[512 * a : 512 * (a + 1), :].rearrange("(p i) r -> p i r", i=PACK)
-            nc.sync.dma_start(out=wu_raw[a][:], in_=rows)
+        load_wu(0, 0, R)
         load_wd_scales(nc.gpsimd, 0, wd4_scales)
         load_wd_scales(nc.sync, 1, wd8_scales)
         load_table(1)
+        load_wu(1, 0, R // 2)
+        load_wu(1, R // 2, R)
         wd8_raw = sb("wd8_raw", [P, N], I32)
         nc.sync.dma_start(out=wd8_raw[:], in_=wd8_words[0].rearrange("p n i -> p (n i)").bitcast(I32))
         sm_sb = sb("sm_sb", [P, PACK], F32)
@@ -107,21 +117,36 @@ def tile_list_modp_silu_res_resbP_kernel(
 
         clear_page(nc.vector, first, third)
 
-        wu_bf = [sb("wu_bf%d" % a, [P, PACK, P, PACK], BF16) for a in range(2)]
+        wu_bf = [sb("wu_bf%d" % a, [P, PACK, P, PACK], BF16, offset=0 if a else None) for a in range(2)]
         wu_q = [sb("wu_q%d" % a, [P, R], U32) for a in range(2)]
         wu_s = [sb("wu_s%d" % a, [P, R], U8) for a in range(2)]
 
         def round_wu(copy, a, r0, r1):
+            base = max(b0 for b0, b1 in wu_loads[a] if b0 <= r0)
+            tile = wu_raw[a, base]
             copy(
                 out=wu_bf[a][:, :, r0 // PACK : r1 // PACK, :].rearrange("p t m i -> p m i t"),
-                in_=wu_raw[a][:, :, r0:r1].rearrange("p i (m t) -> p m i t", t=PACK),
+                in_=tile[:, :, r0 - base : r1 - base].rearrange("p i (m t) -> p m i t", t=PACK),
             )
+
+        wd8 = sb("wd8", [P, N], I32)
+        wd4 = sb("wd4", [P, 2 * N], U8)
+        wd_sc = {}
+
+        def deal(out, in_):
+            nc.vector.tensor_copy(
+                out.rearrange("p (t m) -> p m t", t=PACK), in_.rearrange("p (m t) -> p m t", t=PACK)
+            )
+
+        def deal_scales(tier, offset=None):
+            wd_sc[tier] = sb("wd_sc%d" % tier, [P, N], U8, offset=offset)
+            deal(wd_sc[tier][:], wd_sc_raw[:, tier * N : (tier + 1) * N])
 
         got_sc = sb("got_sc", [P, J], U8)
         got_w = {}
 
-        def gather_words(a, j0, j1):
-            tile = sb("got_w%d_%d" % (a, j0), [P, j1 - j0], U32)
+        def gather_words(a, j0, j1, tag="", offset=None):
+            tile = sb("got_w%d_%d" % (a, j0), [P, j1 - j0], U32, tag=tag, offset=offset)
             nc.vector.tensor_copy(tile[:], tab_w[a][:].bitcast(U32).indirect(listed(j0, j1)))
             for j in range(j0, j1, NARROW):
                 got_w[a, j] = (tile, j0)
@@ -140,12 +165,23 @@ def tile_list_modp_silu_res_resbP_kernel(
         nc.vector.tensor_copy(got_sc[:], tab_sc[:].indirect(offsets[:]))
         gather_words(0, 0, J)
         for a in range(2):
-            round_wu(nc.scalar.copy, a, 0, R // 2)
-            round_wu(nc.vector.tensor_copy, a, R // 2, R)
-            nc.vector.quantize_mx(
-                out=wu_q[a][:].bitcast(FP8X4), scales=wu_s[a][:],
-                in_=wu_bf[a][:].rearrange("p t m i -> p (t m i)"),
-            )
+            if a == 1:
+                gather_words(1, 0, J - QUARTER, "wu_bf0")
+            for r0, r1 in wu_loads[a]:
+                cut = r0 + (r1 - r0) * 3 // 8 if r1 == R else r1
+                round_wu(nc.scalar.copy, a, r0, cut)
+                if cut < r1:
+                    round_wu(nc.vector.tensor_copy, a, cut, r1)
+            step = 2 if a else PACK
+            for t in range(0, PACK, step):
+                cols = slice(t * P, (t + step) * P)
+                nc.vector.quantize_mx(
+                    out=wu_q[a][:, cols].bitcast(FP8X4), scales=wu_s[a][:, cols],
+                    in_=wu_bf[a][:, t : t + step, :, :].rearrange("p t m i -> p (t m i)"),
+                )
+
+        gather_words(1, J - QUARTER, J, offset=0)
+        deal_scales(0, offset=4 * QUARTER)
 
         narrow = [bank_tile("narrow%d" % c, [P, PACK, NARROW], c) for c in range(HALF // NARROW)]
 
@@ -158,6 +194,9 @@ def tile_list_modp_silu_res_resbP_kernel(
 
         for c in range(len(narrow)):
             up_narrow(0, c)
+        wide = [bank_tile("wide%d" % t, [P, HALF], PACK + t) for t in range(PACK)]
+        for t in range(PACK):
+            up_pass(wide[t][:], 0, t, HALF, J, True, False)
 
         h_q = [sb("h_q%d" % u, [P, HALF], U32) for u in range(2)]
         h_s = [sb("h_s%d" % u, [P, HALF], U8) for u in range(2)]
@@ -167,7 +206,7 @@ def tile_list_modp_silu_res_resbP_kernel(
             cols = slice(j0 - u * HALF, j1 - u * HALF)
             nc.vector.quantize_mx(
                 out=h_q[u][:, cols].bitcast(FP8X4), scales=h_s[u][:, cols],
-                in_=h_bf[:].rearrange("p j t -> p (j t)"),
+                in_=h_bf.rearrange("p j t -> p (j t)"),
             )
 
         def hidden_narrow(j0, j1):
@@ -175,12 +214,15 @@ def tile_list_modp_silu_res_resbP_kernel(
             for c in range(j0 // NARROW, j1 // NARROW):
                 up_narrow(1, c)
                 act = sb("act%d" % c, [P, NARROW, PACK], F32)
-                nc.scalar.activation(act[:], narrow[c][:].rearrange("p t j -> p j t"), ACT.Silu)
-                nc.vector.tensor_tensor(
-                    h_bf[:, c * NARROW - j0 : (c + 1) * NARROW - j0, :], act[:],
-                    sm_sb[:].unsqueeze(1).to_broadcast([P, NARROW, PACK]), MULT,
-                )
-            return h_bf
+                step = NARROW if c else NARROW // 2
+                for lo in range(0, NARROW, step):
+                    part = act[:, lo : lo + step, :]
+                    nc.scalar.activation(part, narrow[c][:, :, lo : lo + step].rearrange("p t j -> p j t"), ACT.Silu)
+                    nc.vector.tensor_tensor(
+                        h_bf[:, c * NARROW - j0 + lo : c * NARROW - j0 + lo + step, :], part,
+                        sm_sb[:].unsqueeze(1).to_broadcast([P, step, PACK]), MULT,
+                    )
+            return h_bf[:]
 
         def hidden_wide(j0, j1):
             width = j1 - j0
@@ -188,29 +230,16 @@ def tile_list_modp_silu_res_resbP_kernel(
             h_slices = sb("h_slices", [P, PACK, width], BF16)
             h_bf = sb("h_bf%d" % j0, [P, width, PACK], BF16)
             for t in range(PACK):
-                bank = bank_tile("wide%d" % t, [P, width], t)
-                for a in range(2):
-                    up_pass(bank[:], a, t, j0, j1, a == 0, a == 1)
+                bank = wide[t]
+                for c0 in range(0, width, QUARTER):
+                    up_pass(bank[:, c0 : c0 + QUARTER], 1, t, j0 + c0, j0 + c0 + QUARTER, False, c0 + QUARTER == width)
                 nc.scalar.activation(act[:, t, :], bank[:], ACT.Silu)
                 nc.scalar.activation(h_slices[:, t, :], act[:, t, :], ACT.Copy, scale=sm_sb[:, t : t + 1])
             nc.scalar.copy(
                 out=h_bf[:].rearrange("p (c i) t -> p c t i", i=4),
                 in_=h_slices[:].rearrange("p t (c i) -> p c t i", i=4),
             )
-            return h_bf
-
-        wd8 = sb("wd8", [P, N], I32)
-        wd4 = sb("wd4", [P, 2 * N], U8)
-        wd_sc = {}
-
-        def deal(out, in_):
-            nc.vector.tensor_copy(
-                out.rearrange("p (t m) -> p m t", t=PACK), in_.rearrange("p (m t) -> p m t", t=PACK)
-            )
-
-        def deal_scales(tier, tag=""):
-            wd_sc[tier] = sb("wd_sc%d" % tier, [P, N], U8, tag=tag)
-            deal(wd_sc[tier][:], wd_sc_raw[:, tier * N : (tier + 1) * N])
+            return h_bf[:]
 
         pieces = ((0, QUARTER), (QUARTER, HALF), (HALF, J))
         units = [(t, j0, j1) for j0, j1 in pieces for t in (first, second)]
@@ -249,23 +278,21 @@ def tile_list_modp_silu_res_resbP_kernel(
         deal(wd4[:].bitcast(U16), wd4_raw[:].bitcast(U16))
         deal_scales(1)
         clear_page(nc.gpsimd, second, last, "wd4_raw")
-        for j0, j1 in pieces:
-            gather_words(1, j0, j1)
         h_bf = hidden_narrow(0, QUARTER)
-        deal_scales(0, "act0")
-        quantise_hidden(0, QUARTER, h_bf)
-        down(first, 0, QUARTER, 4)
-        down(second, 0, QUARTER, 5)
+        for c in range(QUARTER // NARROW):
+            quantise_hidden(c * NARROW, (c + 1) * NARROW, h_bf[:, c * NARROW : (c + 1) * NARROW, :])
+        down(first, 0, QUARTER, 0)
+        down(second, 0, QUARTER, 1)
         quantise_hidden(QUARTER, HALF, hidden_narrow(QUARTER, HALF))
-        down(first, QUARTER, HALF, 6)
+        down(first, QUARTER, HALF, 2)
         quantise_hidden(HALF, J, hidden_wide(HALF, J))
         y_sb[held] = sb("y_held", [P, QUARTER], F32, tag="h_slices")
-        down(second, QUARTER, HALF, 7)
+        down(second, QUARTER, HALF, 3)
         down(first, HALF, J, 4)
         down(second, HALF, J, 5)
         down(third, 0, HALF, 6)
-        down(third, HALF, J, 0)
-        down(last, 0, HALF, 7)
+        down(third, HALF, J, 7)
+        down(last, 0, HALF, 0)
         down(last, HALF, J, 1)
 
         out_rows = out_0.rearrange("(p t) c -> p t c", t=PACK)

@@ -26,6 +26,9 @@ QUARTER = J // 4
 SUMS_IN_FLIGHT = 3
 SLICE_ORDER = (0, 2, 1, 3)
 BLOCKS = ((0, 512), (512, 1024), (1024, 1536), (1536, 1792), (1792, 2048))
+WU_LOADS = (((0, R),), ((0, R // 2), (R // 2, R)))
+SCALAR_EIGHTHS_OF_WU = 3
+VECTOR_EIGHTHS_OF_BLOCK = 5
 
 
 def tile_list_modp_silu_res_resbP_kernel(
@@ -60,13 +63,12 @@ def tile_list_modp_silu_res_resbP_kernel(
 
         tab_w = [sb("tab_w%d" % a, [P, T], I32) for a in range(2)]
         wu_raw = {}
-        wu_loads = (((0, R),), ((0, R // 2), (R // 2, R)))
 
-        def load_wu(a, r0, r1):
-            tile = sb("wu_raw%d_%d" % (a, r0), [P, PACK, r1 - r0], F32)
-            rows = wu[512 * a : 512 * (a + 1), r0:r1].rearrange("(p i) r -> p i r", i=PACK)
-            nc.sync.dma_start(out=tile[:], in_=rows)
-            wu_raw[a, r0] = tile
+        def load_wu(a):
+            for r0, r1 in WU_LOADS[a]:
+                wu_raw[a, r0] = sb("wu_raw%d_%d" % (a, r0), [P, PACK, r1 - r0], F32)
+                rows = wu[512 * a : 512 * (a + 1), r0:r1].rearrange("(p i) r -> p i r", i=PACK)
+                nc.sync.dma_start(out=wu_raw[a, r0][:], in_=rows)
 
         def load_table(a):
             nc.sync.dma_start(out=tab_w[a][:], in_=tab_words[a].rearrange("p t i -> p (t i)").bitcast(I32))
@@ -86,12 +88,11 @@ def tile_list_modp_silu_res_resbP_kernel(
                 in_=tab_scales[:, 4 * q : 4 * q + 4, :].bitcast(I32),
             )
         load_table(0)
-        load_wu(0, 0, R)
+        load_wu(0)
         load_wd_scales(nc.gpsimd, 0, wd4_scales)
         load_wd_scales(nc.sync, 1, wd8_scales)
         load_table(1)
-        load_wu(1, 0, R // 2)
-        load_wu(1, R // 2, R)
+        load_wu(1)
         wd8_raw = sb("wd8_raw", [P, N], I32)
         nc.sync.dma_start(out=wd8_raw[:], in_=wd8_words[0].rearrange("p n i -> p (n i)").bitcast(I32))
         sm_sb = sb("sm_sb", [P, PACK], F32)
@@ -121,12 +122,10 @@ def tile_list_modp_silu_res_resbP_kernel(
         wu_q = [sb("wu_q%d" % a, [P, R], U32) for a in range(2)]
         wu_s = [sb("wu_s%d" % a, [P, R], U8) for a in range(2)]
 
-        def round_wu(copy, a, r0, r1):
-            base = max(b0 for b0, b1 in wu_loads[a] if b0 <= r0)
-            tile = wu_raw[a, base]
+        def round_wu(copy, a, base, r0, r1):
             copy(
                 out=wu_bf[a][:, :, r0 // PACK : r1 // PACK, :].rearrange("p t m i -> p m i t"),
-                in_=tile[:, :, r0 - base : r1 - base].rearrange("p i (m t) -> p m i t", t=PACK),
+                in_=wu_raw[a, base][:, :, r0 - base : r1 - base].rearrange("p i (m t) -> p m i t", t=PACK),
             )
 
         wd8 = sb("wd8", [P, N], I32)
@@ -164,22 +163,27 @@ def tile_list_modp_silu_res_resbP_kernel(
 
         nc.vector.tensor_copy(got_sc[:], tab_sc[:].indirect(offsets[:]))
         gather_words(0, 0, J)
-        for a in range(2):
-            if a == 1:
-                gather_words(1, 0, J - QUARTER, "wu_bf0")
-            for r0, r1 in wu_loads[a]:
-                cut = r0 + (r1 - r0) * 3 // 8 if r1 == R else r1
-                round_wu(nc.scalar.copy, a, r0, cut)
-                if cut < r1:
-                    round_wu(nc.vector.tensor_copy, a, cut, r1)
-            step = 2 if a else PACK
-            for t in range(0, PACK, step):
-                cols = slice(t * P, (t + step) * P)
-                nc.vector.quantize_mx(
-                    out=wu_q[a][:, cols].bitcast(FP8X4), scales=wu_s[a][:, cols],
-                    in_=wu_bf[a][:, t : t + step, :, :].rearrange("p t m i -> p (t m i)"),
-                )
 
+        def round_pass(a):
+            for r0, r1 in WU_LOADS[a]:
+                cut = r0 + (r1 - r0) * SCALAR_EIGHTHS_OF_WU // 8 if r1 == R else r1
+                round_wu(nc.scalar.copy, a, r0, r0, cut)
+                if cut < r1:
+                    round_wu(nc.vector.tensor_copy, a, r0, cut, r1)
+
+        def quantise_wu(a, t0, t1):
+            cols = slice(t0 * P, t1 * P)
+            nc.vector.quantize_mx(
+                out=wu_q[a][:, cols].bitcast(FP8X4), scales=wu_s[a][:, cols],
+                in_=wu_bf[a][:, t0:t1, :, :].rearrange("p t m i -> p (t m i)"),
+            )
+
+        round_pass(0)
+        quantise_wu(0, 0, PACK)
+        gather_words(1, 0, J - QUARTER, "wu_bf0")
+        round_pass(1)
+        quantise_wu(1, 0, PACK // 2)
+        quantise_wu(1, PACK // 2, PACK)
         gather_words(1, J - QUARTER, J, offset=0)
         deal_scales(0, offset=4 * QUARTER)
 
@@ -230,10 +234,10 @@ def tile_list_modp_silu_res_resbP_kernel(
             h_slices = sb("h_slices", [P, PACK, width], BF16)
             h_bf = sb("h_bf%d" % j0, [P, width, PACK], BF16)
             for t in range(PACK):
-                bank = wide[t]
                 for c0 in range(0, width, QUARTER):
-                    up_pass(bank[:, c0 : c0 + QUARTER], 1, t, j0 + c0, j0 + c0 + QUARTER, False, c0 + QUARTER == width)
-                nc.scalar.activation(act[:, t, :], bank[:], ACT.Silu)
+                    c1 = c0 + QUARTER
+                    up_pass(wide[t][:, c0:c1], 1, t, j0 + c0, j0 + c1, False, c1 == width)
+                nc.scalar.activation(act[:, t, :], wide[t][:], ACT.Silu)
                 nc.scalar.activation(h_slices[:, t, :], act[:, t, :], ACT.Copy, scale=sm_sb[:, t : t + 1])
             nc.scalar.copy(
                 out=h_bf[:].rearrange("p (c i) t -> p c t i", i=4),
@@ -278,9 +282,9 @@ def tile_list_modp_silu_res_resbP_kernel(
         deal(wd4[:].bitcast(U16), wd4_raw[:].bitcast(U16))
         deal_scales(1)
         clear_page(nc.gpsimd, second, last, "wd4_raw")
-        h_bf = hidden_narrow(0, QUARTER)
-        for c in range(QUARTER // NARROW):
-            quantise_hidden(c * NARROW, (c + 1) * NARROW, h_bf[:, c * NARROW : (c + 1) * NARROW, :])
+        first_h = hidden_narrow(0, QUARTER)
+        for j0 in range(0, QUARTER, NARROW):
+            quantise_hidden(j0, j0 + NARROW, first_h[:, j0 : j0 + NARROW, :])
         down(first, 0, QUARTER, 0)
         down(second, 0, QUARTER, 1)
         quantise_hidden(QUARTER, HALF, hidden_narrow(QUARTER, HALF))
@@ -327,8 +331,9 @@ def tile_list_modp_silu_res_resbP_kernel(
 
         def round_last(g):
             c0, c1 = BLOCKS[g]
-            share = (c1 - c0) // 2
-            nc.vector.tensor_copy(woven[g][:, 0:share, last], page[last][:, c0 : c0 + share])
+            share = (c1 - c0) * VECTOR_EIGHTHS_OF_BLOCK // 8 if c1 - c0 == BANK else 0
+            if share:
+                nc.vector.tensor_copy(woven[g][:, 0:share, last], page[last][:, c0 : c0 + share])
             nc.scalar.copy(out=woven[g][:, share : c1 - c0, last], in_=page[last][:, c0 + share : c1])
 
         round_last(0)

@@ -57,7 +57,7 @@ def tile_list_modp_silu_res_resbP_kernel(
             return offsets[:, j0 // 16 : j1 // 16]
 
         tab_sc = sb("tab_sc", [P, T], U8)
-        nc.gpsimd.memset(tab_sc[:].bitcast(I32), 0)
+        nc.vector.memset(tab_sc[:].bitcast(I32), 0)
         wd_sc_raw = sb("wd_sc_raw", [P, 2 * N], U8)
         nc.vector.memset(wd_sc_raw[:].bitcast(I32), 0)
 

@@ -117,6 +117,7 @@ def tile_list_modp_silu_res_resbP_kernel(
             page[late] = tile
 
         clear_page(nc.vector, first, third)
+        clear_page(nc.vector, second, last)
 
         wu_bf = [sb("wu_bf%d" % a, [P, PACK, P, PACK], BF16, offset=0 if a else None) for a in range(2)]
         wu_q = [sb("wu_q%d" % a, [P, R], U32) for a in range(2)]
@@ -281,7 +282,6 @@ def tile_list_modp_silu_res_resbP_kernel(
         deal(wd8[:], wd8_raw[:])
         deal(wd4[:].bitcast(U16), wd4_raw[:].bitcast(U16))
         deal_scales(1)
-        clear_page(nc.gpsimd, second, last, "wd4_raw")
         first_h = hidden_narrow(0, QUARTER)
         for j0 in range(0, QUARTER, NARROW):
             quantise_hidden(j0, j0 + NARROW, first_h[:, j0 : j0 + NARROW, :])

@@ -26,8 +26,8 @@ QUARTER = J // 4
 SUMS_IN_FLIGHT = 3
 SLICE_ORDER = (0, 2, 1, 3)
 BLOCKS = ((0, 512), (512, 1024), (1024, 1536), (1536, 1792), (1792, 2048))
-WU_LOADS = (((0, R),), ((0, R // 2), (R // 2, R)))
-SCALAR_EIGHTHS_OF_WU = 3
+SCALAR_EIGHTHS_OF_WU = 4
+LATE_GATHERS = ((0, 128), (128, 256), (256, 512), (512, 1024))
 VECTOR_EIGHTHS_OF_BLOCK = 5
 
 
@@ -57,92 +57,84 @@ def tile_list_modp_silu_res_resbP_kernel(
             return offsets[:, j0 // 16 : j1 // 16]
 
         tab_sc = sb("tab_sc", [P, T], U8)
-        nc.vector.memset(tab_sc[:].bitcast(I32), 0)
-        wd_sc_raw = sb("wd_sc_raw", [P, 2 * N], U8)
+        nc.gpsimd.memset(tab_sc[:].bitcast(I32), 0)
+        wd_sc_raw = sb("wd_sc_raw", [P, N], U8)
         nc.vector.memset(wd_sc_raw[:].bitcast(I32), 0)
 
         tab_w = [sb("tab_w%d" % a, [P, T], I32) for a in range(2)]
-        wu_raw = {}
+        wu_raw = [sb("wu_raw%d" % a, [P, PACK, R], F32) for a in range(2)]
 
         def load_wu(a):
-            for r0, r1 in WU_LOADS[a]:
-                wu_raw[a, r0] = sb("wu_raw%d_%d" % (a, r0), [P, PACK, r1 - r0], F32)
-                rows = wu[512 * a : 512 * (a + 1), r0:r1].rearrange("(p i) r -> p i r", i=PACK)
-                nc.sync.dma_start(out=wu_raw[a, r0][:], in_=rows)
+            rows = wu[512 * a : 512 * (a + 1), :].rearrange("(p i) r -> p i r", i=PACK)
+            nc.sync.dma_start(out=wu_raw[a][:], in_=rows)
 
         def load_table(a):
             nc.sync.dma_start(out=tab_w[a][:], in_=tab_words[a].rearrange("p t i -> p (t i)").bitcast(I32))
 
-        def load_wd_scales(queue, tier, scales):
+        def load_wd_scales(tier, scales):
             for q in range(4):
-                queue.dma_start(
-                    out=wd_sc_raw[32 * q : 32 * q + 4, tier * N : (tier + 1) * N].bitcast(I32),
+                first_row = 32 * q + 4 * tier
+                nc.sync.dma_start(
+                    out=wd_sc_raw[first_row : first_row + 4, :].bitcast(I32),
                     in_=scales[0, 4 * q : 4 * q + 4, :].bitcast(I32),
                 )
 
-        wd4_raw = sb("wd4_raw", [P, 2 * N], U8)
-        nc.sync.dma_start(out=wd4_raw[:].bitcast(I32), in_=wd4_words[0].bitcast(I32))
         for q in range(4):
-            nc.sync.dma_start(
+            nc.gpsimd.dma_start(
                 out=tab_sc[32 * q : 32 * q + 8, :].bitcast(I32),
                 in_=tab_scales[:, 4 * q : 4 * q + 4, :].bitcast(I32),
             )
         load_table(0)
         load_wu(0)
-        load_wd_scales(nc.gpsimd, 0, wd4_scales)
-        load_wd_scales(nc.sync, 1, wd8_scales)
-        load_table(1)
-        load_wu(1)
-        wd8_raw = sb("wd8_raw", [P, N], I32)
-        nc.sync.dma_start(out=wd8_raw[:], in_=wd8_words[0].rearrange("p n i -> p (n i)").bitcast(I32))
         sm_sb = sb("sm_sb", [P, PACK], F32)
         nc.sync.dma_start(out=sm_sb[:], in_=sm.rearrange("(p t) -> p t", t=PACK))
         b_sb = sb("b_sb", [P, PACK], F32)
         nc.sync.dma_start(out=b_sb[:], in_=b.rearrange("(p t) -> p t", t=PACK))
+        load_wd_scales(1, wd8_scales)
+        load_wu(1)
+        load_table(1)
+        wd4_raw = sb("wd4_raw", [P, 2 * N], U8)
+        nc.sync.dma_start(out=wd4_raw[:].bitcast(I32), in_=wd4_words[0].bitcast(I32))
+        wd8_raw = sb("wd8_raw", [P, N], I32)
+        nc.sync.dma_start(out=wd8_raw[:], in_=wd8_words[0].rearrange("p n i -> p (n i)").bitcast(I32))
+        load_wd_scales(0, wd4_scales)
         res = {t: sb("res%d" % t, [P, T], F32) for t in SLICE_ORDER}
         res_rows = rT.rearrange("(p t) c -> p t c", t=PACK)
-        for t in (first, second):
-            nc.sync.dma_start(out=res[t][:], in_=res_rows[:, t, :])
         wgo_sb = sb("wgo_sb", [P, J], F32)
-        nc.sync.dma_start(out=wgo_sb[:], in_=wgo)
+        for t, cols in ((first, slice(0, QUARTER)), (second, slice(QUARTER, J))):
+            nc.sync.dma_start(out=res[t][:], in_=res_rows[:, t, :])
+            nc.sync.dma_start(out=wgo_sb[:, cols], in_=wgo[:, cols])
         for t in (third, last):
             nc.sync.dma_start(out=res[t][:], in_=res_rows[:, t, :])
 
         page = {}
 
-        def clear_page(engine, early, late, tag=""):
-            tile = sb("page%d" % early, [P, T], F32, tag=tag)
-            engine.memset(tile[:].bitcast(I32), 0)
+        def clear_page(early, late):
+            tile = sb("page%d" % early, [P, T], F32)
+            for c0, c1 in ((0, T // 2 - 1), (T // 2 - 1, T)):
+                nc.vector.memset(tile[:, c0:c1].bitcast(I32), 0)
             page[early] = tile
             page[late] = tile
 
-        clear_page(nc.vector, first, third)
-        clear_page(nc.vector, second, last)
+        clear_page(first, third)
+        clear_page(second, last)
 
         wu_bf = [sb("wu_bf%d" % a, [P, PACK, P, PACK], BF16, offset=0 if a else None) for a in range(2)]
         wu_q = [sb("wu_q%d" % a, [P, R], U32) for a in range(2)]
         wu_s = [sb("wu_s%d" % a, [P, R], U8) for a in range(2)]
 
-        def round_wu(copy, a, base, r0, r1):
+        def round_wu(copy, a, r0, r1):
             copy(
                 out=wu_bf[a][:, :, r0 // PACK : r1 // PACK, :].rearrange("p t m i -> p m i t"),
-                in_=wu_raw[a, base][:, :, r0 - base : r1 - base].rearrange("p i (m t) -> p m i t", t=PACK),
+                in_=wu_raw[a][:, :, r0:r1].rearrange("p i (m t) -> p m i t", t=PACK),
             )
 
         wd8 = sb("wd8", [P, N], I32)
         wd4 = sb("wd4", [P, 2 * N], U8)
-        wd_sc = {}
 
-        def deal(out, in_):
-            nc.vector.tensor_copy(
-                out.rearrange("p (t m) -> p m t", t=PACK), in_.rearrange("p (m t) -> p m t", t=PACK)
-            )
+        def deal(copy, out, in_):
+            copy(out=out.rearrange("p (t m) -> p m t", t=PACK), in_=in_.rearrange("p (m t) -> p m t", t=PACK))
 
-        def deal_scales(tier, offset=None):
-            wd_sc[tier] = sb("wd_sc%d" % tier, [P, N], U8, offset=offset)
-            deal(wd_sc[tier][:], wd_sc_raw[:, tier * N : (tier + 1) * N])
-
-        got_sc = sb("got_sc", [P, J], U8)
         got_w = {}
 
         def gather_words(a, j0, j1, tag="", offset=None):
@@ -162,15 +154,9 @@ def tile_list_modp_silu_res_resbP_kernel(
                 start=start, stop=stop,
             )
 
-        nc.vector.tensor_copy(got_sc[:], tab_sc[:].indirect(offsets[:]))
         gather_words(0, 0, J)
-
-        def round_pass(a):
-            for r0, r1 in WU_LOADS[a]:
-                cut = r0 + (r1 - r0) * SCALAR_EIGHTHS_OF_WU // 8 if r1 == R else r1
-                round_wu(nc.scalar.copy, a, r0, r0, cut)
-                if cut < r1:
-                    round_wu(nc.vector.tensor_copy, a, r0, cut, r1)
+        got_sc = sb("got_sc", [P, J], U8, tag="tab_w0")
+        nc.vector.tensor_copy(got_sc[:], tab_sc[:].indirect(offsets[:]))
 
         def quantise_wu(a, t0, t1):
             cols = slice(t0 * P, t1 * P)
@@ -179,14 +165,16 @@ def tile_list_modp_silu_res_resbP_kernel(
                 in_=wu_bf[a][:, t0:t1, :, :].rearrange("p t m i -> p (t m i)"),
             )
 
-        round_pass(0)
+        round_wu(nc.scalar.copy, 0, 0, R)
         quantise_wu(0, 0, PACK)
-        gather_words(1, 0, J - QUARTER, "wu_bf0")
-        round_pass(1)
-        quantise_wu(1, 0, PACK // 2)
-        quantise_wu(1, PACK // 2, PACK)
-        gather_words(1, J - QUARTER, J, offset=0)
-        deal_scales(0, offset=4 * QUARTER)
+        cut = R * SCALAR_EIGHTHS_OF_WU // 8
+        round_wu(nc.scalar.copy, 1, 0, cut)
+        round_wu(nc.vector.tensor_copy, 1, cut, R)
+        quantise_wu(1, 0, PACK)
+        for j0, j1 in LATE_GATHERS:
+            gather_words(1, j0, j1, offset=4 * j0)
+        wd_sc = sb("wd_sc", [P, N], U8)
+        deal(nc.vector.tensor_copy, wd_sc[:], wd_sc_raw[:])
 
         narrow = [bank_tile("narrow%d" % c, [P, PACK, NARROW], c) for c in range(HALF // NARROW)]
 
@@ -200,8 +188,6 @@ def tile_list_modp_silu_res_resbP_kernel(
         for c in range(len(narrow)):
             up_narrow(0, c)
         wide = [bank_tile("wide%d" % t, [P, HALF], PACK + t) for t in range(PACK)]
-        for t in range(PACK):
-            up_pass(wide[t][:], 0, t, HALF, J, True, False)
 
         h_q = [sb("h_q%d" % u, [P, HALF], U32) for u in range(2)]
         h_s = [sb("h_s%d" % u, [P, HALF], U8) for u in range(2)]
@@ -235,9 +221,8 @@ def tile_list_modp_silu_res_resbP_kernel(
             h_slices = sb("h_slices", [P, PACK, width], BF16)
             h_bf = sb("h_bf%d" % j0, [P, width, PACK], BF16)
             for t in range(PACK):
-                for c0 in range(0, width, QUARTER):
-                    c1 = c0 + QUARTER
-                    up_pass(wide[t][:, c0:c1], 1, t, j0 + c0, j0 + c1, False, c1 == width)
+                up_pass(wide[t][:], 1, t, j0, j1, True, False)
+                up_pass(wide[t][:], 0, t, j0, j1, False, True)
                 nc.scalar.activation(act[:, t, :], wide[t][:], ACT.Silu)
                 nc.scalar.activation(h_slices[:, t, :], act[:, t, :], ACT.Copy, scale=sm_sb[:, t : t + 1])
             nc.scalar.copy(
@@ -266,23 +251,22 @@ def tile_list_modp_silu_res_resbP_kernel(
                 nc.tensor.matmul_mx(
                     out=bank[:, c0 : c0 + step],
                     lhsT=wd4[:, 2 * t * P : 2 * (t + 1) * P].bitcast(FP4X4),
-                    lhsT_scale=wd_sc[0][:, t * P : (t + 1) * P],
+                    lhsT_scale=wd_sc[:, t * P : (t + 1) * P],
                     rhs=h_q[u][:, cols].bitcast(FP8X4), rhs_scale=h_s[u][:, cols],
                     start=True, stop=False,
                 )
                 nc.tensor.matmul_mx(
                     out=bank[:, c0 : c0 + step],
                     lhsT=wd8[:, t * P : (t + 1) * P].bitcast(FP8X4),
-                    lhsT_scale=wd_sc[1][:, t * P : (t + 1) * P],
+                    lhsT_scale=wd_sc[4:P, t * P : (t + 1) * P],
                     rhs=h_q[u][:, cols].bitcast(FP8X4), rhs_scale=h_s[u][:, cols],
                     start=False, stop=True,
                 )
             nc.scalar.activation(y_view(t, j0, j1), bank[:], ACT.Identity, bias=b_sb[:, t : t + 1])
 
-        deal(wd8[:], wd8_raw[:])
-        deal(wd4[:].bitcast(U16), wd4_raw[:].bitcast(U16))
-        deal_scales(1)
         first_h = hidden_narrow(0, QUARTER)
+        deal(nc.scalar.copy, wd4[:].bitcast(U16), wd4_raw[:].bitcast(U16))
+        deal(nc.scalar.copy, wd8[:].bitcast(U32), wd8_raw[:].bitcast(U32))
         for j0 in range(0, QUARTER, NARROW):
             quantise_hidden(j0, j0 + NARROW, first_h[:, j0 : j0 + NARROW, :])
         down(first, 0, QUARTER, 0)

@@ -26,8 +26,15 @@ QUARTER = J // 4
 SUMS_IN_FLIGHT = 3
 SLICE_ORDER = (0, 2, 1, 3)
 BLOCKS = ((0, 512), (512, 1024), (1024, 1536), (1536, 1792), (1792, 2048))
-SCALAR_EIGHTHS_OF_WU = 4
-LATE_GATHERS = ((0, 128), (128, 256), (256, 512), (512, 1024))
+WU_LOADS = (((0, R),), ((0, R // 2), (R // 2, R)))
+SCALAR_EIGHTHS_OF_WU = (5, 3)
+TABLE_LEAD = 256
+LATE_GATHER = 256
+WIDE_AHEAD = 1
+LATE_BANKS = {1: 5, 2: 6, 3: 7}
+RAW_WD = 0
+ROUNDED_WU = RAW_WD + 8 * N
+LAST_ACT = ROUNDED_WU + 10 * N
 VECTOR_EIGHTHS_OF_BLOCK = 5
 
 
@@ -56,77 +63,86 @@ def tile_list_modp_silu_res_resbP_kernel(
         def listed(j0, j1):
             return offsets[:, j0 // 16 : j1 // 16]
 
+        warm_in = sb("warm_in", [P, 1], F32)
+        nc.gpsimd.memset(warm_in[:], 0.0)
+        warm_out = sb("warm_out", [P, 1], F32)
+        nc.scalar.activation(warm_out[:], warm_in[:], ACT.Silu)
+
         tab_sc = sb("tab_sc", [P, T], U8)
-        nc.gpsimd.memset(tab_sc[:].bitcast(I32), 0)
+        nc.vector.memset(tab_sc[:].bitcast(I32), 0)
         wd_sc_raw = sb("wd_sc_raw", [P, N], U8)
         nc.vector.memset(wd_sc_raw[:].bitcast(I32), 0)
 
         tab_w = [sb("tab_w%d" % a, [P, T], I32) for a in range(2)]
-        wu_raw = [sb("wu_raw%d" % a, [P, PACK, R], F32) for a in range(2)]
+        wu_raw = {}
 
         def load_wu(a):
-            rows = wu[512 * a : 512 * (a + 1), :].rearrange("(p i) r -> p i r", i=PACK)
-            nc.sync.dma_start(out=wu_raw[a][:], in_=rows)
+            for r0, r1 in WU_LOADS[a]:
+                wu_raw[a, r0] = sb("wu_raw%d_%d" % (a, r0), [P, PACK, r1 - r0], F32)
+                rows = wu[512 * a : 512 * (a + 1), r0:r1].rearrange("(p i) r -> p i r", i=PACK)
+                nc.sync.dma_start(out=wu_raw[a, r0][:], in_=rows)
 
-        def load_table(a):
-            nc.sync.dma_start(out=tab_w[a][:], in_=tab_words[a].rearrange("p t i -> p (t i)").bitcast(I32))
+        def load_table(a, c0, c1):
+            words = tab_words[a].rearrange("p t i -> p (t i)").bitcast(I32)
+            nc.sync.dma_start(out=tab_w[a][:, c0:c1], in_=words[:, c0:c1])
 
-        def load_wd_scales(tier, scales):
+        def load_wd_scales(queue, tier, scales):
             for q in range(4):
                 first_row = 32 * q + 4 * tier
-                nc.sync.dma_start(
+                queue.dma_start(
                     out=wd_sc_raw[first_row : first_row + 4, :].bitcast(I32),
                     in_=scales[0, 4 * q : 4 * q + 4, :].bitcast(I32),
                 )
 
+        load_table(0, 0, TABLE_LEAD)
         for q in range(4):
-            nc.gpsimd.dma_start(
+            nc.sync.dma_start(
                 out=tab_sc[32 * q : 32 * q + 8, :].bitcast(I32),
                 in_=tab_scales[:, 4 * q : 4 * q + 4, :].bitcast(I32),
             )
-        load_table(0)
+        load_table(0, TABLE_LEAD, T)
         load_wu(0)
+        load_wd_scales(nc.gpsimd, 0, wd4_scales)
+        load_wd_scales(nc.sync, 1, wd8_scales)
+        load_table(1, 0, T)
+        load_wu(1)
+        wd8_raw = sb("wd8_raw", [P, N], I32, offset=RAW_WD)
+        nc.sync.dma_start(out=wd8_raw[:], in_=wd8_words[0].rearrange("p n i -> p (n i)").bitcast(I32))
+        wd4_raw = sb("wd4_raw", [P, 2 * N], U8, offset=RAW_WD + 4 * N)
+        nc.sync.dma_start(out=wd4_raw[:].bitcast(I32), in_=wd4_words[0].bitcast(I32))
         sm_sb = sb("sm_sb", [P, PACK], F32)
         nc.sync.dma_start(out=sm_sb[:], in_=sm.rearrange("(p t) -> p t", t=PACK))
         b_sb = sb("b_sb", [P, PACK], F32)
         nc.sync.dma_start(out=b_sb[:], in_=b.rearrange("(p t) -> p t", t=PACK))
-        load_wd_scales(1, wd8_scales)
-        load_wu(1)
-        load_table(1)
-        wd4_raw = sb("wd4_raw", [P, 2 * N], U8)
-        nc.sync.dma_start(out=wd4_raw[:].bitcast(I32), in_=wd4_words[0].bitcast(I32))
-        wd8_raw = sb("wd8_raw", [P, N], I32)
-        nc.sync.dma_start(out=wd8_raw[:], in_=wd8_words[0].rearrange("p n i -> p (n i)").bitcast(I32))
-        load_wd_scales(0, wd4_scales)
         res = {t: sb("res%d" % t, [P, T], F32) for t in SLICE_ORDER}
         res_rows = rT.rearrange("(p t) c -> p t c", t=PACK)
         wgo_sb = sb("wgo_sb", [P, J], F32)
-        for t, cols in ((first, slice(0, QUARTER)), (second, slice(QUARTER, J))):
-            nc.sync.dma_start(out=res[t][:], in_=res_rows[:, t, :])
-            nc.sync.dma_start(out=wgo_sb[:, cols], in_=wgo[:, cols])
+        nc.sync.dma_start(out=res[first][:], in_=res_rows[:, first, :])
+        nc.sync.dma_start(out=res[second][:], in_=res_rows[:, second, :])
+        nc.sync.dma_start(out=wgo_sb[:, 0:QUARTER], in_=wgo[:, 0:QUARTER])
+        nc.sync.dma_start(out=wgo_sb[:, QUARTER:J], in_=wgo[:, QUARTER:J])
         for t in (third, last):
             nc.sync.dma_start(out=res[t][:], in_=res_rows[:, t, :])
 
         page = {}
 
-        def clear_page(early, late):
+        def clear_page(engine, early, late):
             tile = sb("page%d" % early, [P, T], F32)
-            for c0, c1 in ((0, T // 2 - 1), (T // 2 - 1, T)):
-                nc.vector.memset(tile[:, c0:c1].bitcast(I32), 0)
+            engine.memset(tile[:].bitcast(I32), 0)
             page[early] = tile
             page[late] = tile
 
-        clear_page(first, third)
-        clear_page(second, last)
+        clear_page(nc.vector, first, third)
+        clear_page(nc.vector, second, last)
 
-        wu_bf = [sb("wu_bf%d" % a, [P, PACK, P, PACK], BF16, offset=0 if a else None) for a in range(2)]
+        wu_bf = [sb("wu_bf%d" % a, [P, PACK, P, PACK], BF16, offset=ROUNDED_WU if a else None) for a in range(2)]
         wu_q = [sb("wu_q%d" % a, [P, R], U32) for a in range(2)]
         wu_s = [sb("wu_s%d" % a, [P, R], U8) for a in range(2)]
 
-        def round_wu(copy, a, r0, r1):
+        def round_wu(copy, a, base, r0, r1):
             copy(
                 out=wu_bf[a][:, :, r0 // PACK : r1 // PACK, :].rearrange("p t m i -> p m i t"),
-                in_=wu_raw[a][:, :, r0:r1].rearrange("p i (m t) -> p m i t", t=PACK),
+                in_=wu_raw[a, base][:, :, r0 - base : r1 - base].rearrange("p i (m t) -> p m i t", t=PACK),
             )
 
         wd8 = sb("wd8", [P, N], I32)
@@ -154,9 +170,9 @@ def tile_list_modp_silu_res_resbP_kernel(
                 start=start, stop=stop,
             )
 
-        gather_words(0, 0, J)
-        got_sc = sb("got_sc", [P, J], U8, tag="tab_w0")
+        got_sc = sb("got_sc", [P, J], U8)
         nc.vector.tensor_copy(got_sc[:], tab_sc[:].indirect(offsets[:]))
+        gather_words(0, 0, J)
 
         def quantise_wu(a, t0, t1):
             cols = slice(t0 * P, t1 * P)
@@ -165,31 +181,41 @@ def tile_list_modp_silu_res_resbP_kernel(
                 in_=wu_bf[a][:, t0:t1, :, :].rearrange("p t m i -> p (t m i)"),
             )
 
-        round_wu(nc.scalar.copy, 0, 0, R)
+        def round_pass(a):
+            for r0, r1 in WU_LOADS[a]:
+                cut = r0 + (r1 - r0) * SCALAR_EIGHTHS_OF_WU[a] // 8 if r1 == R else r1
+                round_wu(nc.scalar.copy, a, r0, r0, cut)
+                if cut < r1:
+                    round_wu(nc.vector.tensor_copy, a, r0, cut, r1)
+
+        round_pass(0)
         quantise_wu(0, 0, PACK)
-        cut = R * SCALAR_EIGHTHS_OF_WU // 8
-        round_wu(nc.scalar.copy, 1, 0, cut)
-        round_wu(nc.vector.tensor_copy, 1, cut, R)
-        quantise_wu(1, 0, PACK)
-        for j0, j1 in LATE_GATHERS:
-            gather_words(1, j0, j1, offset=4 * j0)
-        wd_sc = sb("wd_sc", [P, N], U8)
+        gather_words(1, 0, J - LATE_GATHER, "wu_bf0")
+        round_pass(1)
+        quantise_wu(1, 0, PACK // 2)
+        quantise_wu(1, PACK // 2, PACK)
+        gather_words(1, J - LATE_GATHER, J, offset=ROUNDED_WU)
+        deal(nc.scalar.copy, wd8[:].bitcast(U32), wd8_raw[:].bitcast(U32))
+        deal(nc.vector.tensor_copy, wd4[:].bitcast(U16), wd4_raw[:].bitcast(U16))
+        wd_sc = sb("wd_sc", [P, N], U8, offset=ROUNDED_WU + 4 * LATE_GATHER)
         deal(nc.vector.tensor_copy, wd_sc[:], wd_sc_raw[:])
 
         narrow = [bank_tile("narrow%d" % c, [P, PACK, NARROW], c) for c in range(HALF // NARROW)]
 
-        def up_narrow(a, c):
+        def up_narrow(a, c, opens):
             for t in range(PACK):
                 up_pass(
                     narrow[c][:, t, :], a, t, c * NARROW, (c + 1) * NARROW,
-                    a == 0 and t == 0, a == 1 and t == PACK - 1,
+                    opens and t == 0, not opens and t == PACK - 1,
                 )
 
         for c in range(len(narrow)):
-            up_narrow(0, c)
-        wide = [bank_tile("wide%d" % t, [P, HALF], PACK + t) for t in range(PACK)]
+            up_narrow(0, c, True)
+        wide = {t: bank_tile("wide", [P, HALF], PACK + t) for t in range(WIDE_AHEAD)}
+        for t in range(WIDE_AHEAD):
+            up_pass(wide[t][:], 0, t, HALF, J, True, False)
 
-        h_q = [sb("h_q%d" % u, [P, HALF], U32) for u in range(2)]
+        h_q = [sb("h_q%d" % u, [P, HALF], U32, tag="" if u else "wd_sc_raw") for u in range(2)]
         h_s = [sb("h_s%d" % u, [P, HALF], U8) for u in range(2)]
 
         def quantise_hidden(j0, j1, h_bf):
@@ -200,11 +226,11 @@ def tile_list_modp_silu_res_resbP_kernel(
                 in_=h_bf.rearrange("p j t -> p (j t)"),
             )
 
-        def hidden_narrow(j0, j1):
-            h_bf = sb("h_bf%d" % j0, [P, j1 - j0, PACK], BF16)
+        def hidden_narrow(j0, j1, offset=None):
+            h_bf = sb("h_bf%d" % j0, [P, j1 - j0, PACK], BF16, offset=offset)
             for c in range(j0 // NARROW, j1 // NARROW):
-                up_narrow(1, c)
-                act = sb("act%d" % c, [P, NARROW, PACK], F32)
+                up_narrow(1, c, False)
+                act = sb("act%d" % c, [P, NARROW, PACK], F32, offset={0: RAW_WD, 3: LAST_ACT}.get(c))
                 step = NARROW if c else NARROW // 2
                 for lo in range(0, NARROW, step):
                     part = act[:, lo : lo + step, :]
@@ -217,14 +243,20 @@ def tile_list_modp_silu_res_resbP_kernel(
 
         def hidden_wide(j0, j1):
             width = j1 - j0
-            act = sb("act_slices", [P, PACK, width], F32)
-            h_slices = sb("h_slices", [P, PACK, width], BF16)
+            act = [sb("act_slice%d" % t, [P, width], F32, offset=LAST_ACT - 2 * N if t == 1 else None) for t in range(PACK)]
+            h_slices = sb("h_slices", [P, PACK, width], BF16, offset=LAST_ACT + 2 * N)
             h_bf = sb("h_bf%d" % j0, [P, width, PACK], BF16)
             for t in range(PACK):
-                up_pass(wide[t][:], 1, t, j0, j1, True, False)
-                up_pass(wide[t][:], 0, t, j0, j1, False, True)
-                nc.scalar.activation(act[:, t, :], wide[t][:], ACT.Silu)
-                nc.scalar.activation(h_slices[:, t, :], act[:, t, :], ACT.Copy, scale=sm_sb[:, t : t + 1])
+                cut = width - LATE_GATHER
+                ahead = t < WIDE_AHEAD
+                if not ahead:
+                    wide[t] = bank_tile("wide", [P, width], LATE_BANKS[t])
+                up_pass(wide[t][:, 0:cut], 1, t, j0, j0 + cut, not ahead, False)
+                up_pass(wide[t][:, cut:width], 1, t, j0 + cut, j1, False, ahead)
+                if not ahead:
+                    up_pass(wide[t][:], 0, t, j0, j1, False, True)
+                nc.scalar.activation(act[t][:], wide[t][:], ACT.Silu)
+                nc.scalar.activation(h_slices[:, t, :], act[t][:], ACT.Copy, scale=sm_sb[:, t : t + 1])
             nc.scalar.copy(
                 out=h_bf[:].rearrange("p (c i) t -> p c t i", i=4),
                 in_=h_slices[:].rearrange("p t (c i) -> p c t i", i=4),
@@ -264,31 +296,30 @@ def tile_list_modp_silu_res_resbP_kernel(
                 )
             nc.scalar.activation(y_view(t, j0, j1), bank[:], ACT.Identity, bias=b_sb[:, t : t + 1])
 
-        first_h = hidden_narrow(0, QUARTER)
-        deal(nc.scalar.copy, wd4[:].bitcast(U16), wd4_raw[:].bitcast(U16))
-        deal(nc.scalar.copy, wd8[:].bitcast(U32), wd8_raw[:].bitcast(U32))
-        for j0 in range(0, QUARTER, NARROW):
-            quantise_hidden(j0, j0 + NARROW, first_h[:, j0 : j0 + NARROW, :])
-        down(first, 0, QUARTER, 0)
-        down(second, 0, QUARTER, 1)
-        quantise_hidden(QUARTER, HALF, hidden_narrow(QUARTER, HALF))
-        down(first, QUARTER, HALF, 2)
+        first_h = [hidden_narrow(0, NARROW, RAW_WD + 4 * N), hidden_narrow(NARROW, QUARTER)]
+        for c, h_bank in enumerate(first_h):
+            quantise_hidden(c * NARROW, (c + 1) * NARROW, h_bank)
+        down(first, 0, QUARTER, 6)
+        down(second, 0, QUARTER, 7)
+        quantise_hidden(QUARTER, HALF, hidden_narrow(QUARTER, HALF, RAW_WD + 4 * N))
+        down(first, QUARTER, HALF, 0)
         quantise_hidden(HALF, J, hidden_wide(HALF, J))
-        y_sb[held] = sb("y_held", [P, QUARTER], F32, tag="h_slices")
-        down(second, QUARTER, HALF, 3)
-        down(first, HALF, J, 4)
-        down(second, HALF, J, 5)
-        down(third, 0, HALF, 6)
-        down(third, HALF, J, 7)
-        down(last, 0, HALF, 0)
-        down(last, HALF, J, 1)
+        y_sb[held] = sb("y_held", [P, QUARTER], F32, offset=LAST_ACT + 2 * N)
+        down(second, QUARTER, HALF, 1)
+        down(first, HALF, J, 2)
+        down(second, HALF, J, 3)
+        down(third, 0, HALF, 4)
+        down(third, HALF, J, 5)
+        down(last, 0, HALF, 6)
+        down(last, HALF, J, 7)
 
         out_rows = out_0.rearrange("(p t) c -> p t c", t=PACK)
         woven = [sb("woven%d" % g, [P, c1 - c0, PACK], BF16) for g, (c0, c1) in enumerate(BLOCKS)]
         ring = sb("ring", [P, SUMS_IN_FLIGHT, J], F32)
 
         def unit_sum(k):
-            return ring[:, k % SUMS_IN_FLIGHT, 0 : units[k][2] - units[k][1]]
+            place = k if k < 2 else (k + 1) % SUMS_IN_FLIGHT
+            return ring[:, place, 0 : units[k][2] - units[k][1]]
 
         def add_residual(k):
             t, j0, j1 = units[k]

@@ -23,18 +23,17 @@ BANK = 512
 NARROW = BANK // PACK
 HALF = J // 2
 QUARTER = J // 4
-SUMS_IN_FLIGHT = 3
 SLICE_ORDER = (0, 2, 1, 3)
 BLOCKS = ((0, 512), (512, 1024), (1024, 1536), (1536, 1792), (1792, 2048))
-WU_LOADS = (((0, R),), ((0, R // 2), (R // 2, R)))
 SCALAR_EIGHTHS_OF_WU = (5, 3)
 TABLE_LEAD = 256
-LATE_GATHER = 256
+LATE_GATHERS = ((0, 128), (128, 256), (256, 512), (512, 1024))
 WIDE_AHEAD = 1
 LATE_BANKS = {1: 5, 2: 6, 3: 7}
 RAW_WD = 0
 ROUNDED_WU = RAW_WD + 8 * N
 LAST_ACT = ROUNDED_WU + 10 * N
+FIRST_H = LAST_ACT + 10 * N
 VECTOR_EIGHTHS_OF_BLOCK = 5
 
 
@@ -64,23 +63,21 @@ def tile_list_modp_silu_res_resbP_kernel(
             return offsets[:, j0 // 16 : j1 // 16]
 
         warm_in = sb("warm_in", [P, 1], F32)
-        nc.gpsimd.memset(warm_in[:], 0.0)
+        nc.vector.memset(warm_in[:], 0.0)
         warm_out = sb("warm_out", [P, 1], F32)
         nc.scalar.activation(warm_out[:], warm_in[:], ACT.Silu)
 
         tab_sc = sb("tab_sc", [P, T], U8)
-        nc.vector.memset(tab_sc[:].bitcast(I32), 0)
+        nc.gpsimd.memset(tab_sc[:].bitcast(I32), 0)
         wd_sc_raw = sb("wd_sc_raw", [P, N], U8)
         nc.vector.memset(wd_sc_raw[:].bitcast(I32), 0)
 
         tab_w = [sb("tab_w%d" % a, [P, T], I32) for a in range(2)]
-        wu_raw = {}
+        wu_raw = [sb("wu_raw%d" % a, [P, PACK, R], F32) for a in range(2)]
 
         def load_wu(a):
-            for r0, r1 in WU_LOADS[a]:
-                wu_raw[a, r0] = sb("wu_raw%d_%d" % (a, r0), [P, PACK, r1 - r0], F32)
-                rows = wu[512 * a : 512 * (a + 1), r0:r1].rearrange("(p i) r -> p i r", i=PACK)
-                nc.sync.dma_start(out=wu_raw[a, r0][:], in_=rows)
+            rows = wu[512 * a : 512 * (a + 1), :].rearrange("(p i) r -> p i r", i=PACK)
+            nc.sync.dma_start(out=wu_raw[a][:], in_=rows)
 
         def load_table(a, c0, c1):
             words = tab_words[a].rearrange("p t i -> p (t i)").bitcast(I32)
@@ -104,8 +101,8 @@ def tile_list_modp_silu_res_resbP_kernel(
         load_wu(0)
         load_wd_scales(nc.gpsimd, 0, wd4_scales)
         load_wd_scales(nc.sync, 1, wd8_scales)
-        load_table(1, 0, T)
         load_wu(1)
+        load_table(1, 0, T)
         wd8_raw = sb("wd8_raw", [P, N], I32, offset=RAW_WD)
         nc.sync.dma_start(out=wd8_raw[:], in_=wd8_words[0].rearrange("p n i -> p (n i)").bitcast(I32))
         wd4_raw = sb("wd4_raw", [P, 2 * N], U8, offset=RAW_WD + 4 * N)
@@ -120,29 +117,30 @@ def tile_list_modp_silu_res_resbP_kernel(
         nc.sync.dma_start(out=res[first][:], in_=res_rows[:, first, :])
         nc.sync.dma_start(out=res[second][:], in_=res_rows[:, second, :])
         nc.sync.dma_start(out=wgo_sb[:, 0:QUARTER], in_=wgo[:, 0:QUARTER])
+        nc.sync.dma_start(out=res[third][:], in_=res_rows[:, third, :])
         nc.sync.dma_start(out=wgo_sb[:, QUARTER:J], in_=wgo[:, QUARTER:J])
-        for t in (third, last):
-            nc.sync.dma_start(out=res[t][:], in_=res_rows[:, t, :])
+        nc.sync.dma_start(out=res[last][:], in_=res_rows[:, last, :])
 
         page = {}
 
-        def clear_page(engine, early, late):
+        def clear_page(engine, early, late, cuts=()):
             tile = sb("page%d" % early, [P, T], F32)
-            engine.memset(tile[:].bitcast(I32), 0)
+            for c0, c1 in zip((0,) + cuts, cuts + (T,)):
+                engine.memset(tile[:, c0:c1].bitcast(I32), 0)
             page[early] = tile
             page[late] = tile
 
-        clear_page(nc.vector, first, third)
+        clear_page(nc.vector, first, third, (T // 2 - 1, T // 2))
         clear_page(nc.vector, second, last)
 
-        wu_bf = [sb("wu_bf%d" % a, [P, PACK, P, PACK], BF16, offset=ROUNDED_WU if a else None) for a in range(2)]
+        wu_bf = [sb("wu_bf%d" % a, [P, PACK, P, PACK], BF16, offset=ROUNDED_WU) for a in range(2)]
         wu_q = [sb("wu_q%d" % a, [P, R], U32) for a in range(2)]
         wu_s = [sb("wu_s%d" % a, [P, R], U8) for a in range(2)]
 
-        def round_wu(copy, a, base, r0, r1):
+        def round_wu(copy, a, r0, r1):
             copy(
                 out=wu_bf[a][:, :, r0 // PACK : r1 // PACK, :].rearrange("p t m i -> p m i t"),
-                in_=wu_raw[a, base][:, :, r0 - base : r1 - base].rearrange("p i (m t) -> p m i t", t=PACK),
+                in_=wu_raw[a][:, :, r0:r1].rearrange("p i (m t) -> p m i t", t=PACK),
             )
 
         wd8 = sb("wd8", [P, N], I32)
@@ -153,8 +151,8 @@ def tile_list_modp_silu_res_resbP_kernel(
 
         got_w = {}
 
-        def gather_words(a, j0, j1, tag="", offset=None):
-            tile = sb("got_w%d_%d" % (a, j0), [P, j1 - j0], U32, tag=tag, offset=offset)
+        def gather_words(a, j0, j1):
+            tile = sb("got_w%d_%d" % (a, j0), [P, j1 - j0], U32)
             nc.vector.tensor_copy(tile[:], tab_w[a][:].bitcast(U32).indirect(listed(j0, j1)))
             for j in range(j0, j1, NARROW):
                 got_w[a, j] = (tile, j0)
@@ -182,23 +180,17 @@ def tile_list_modp_silu_res_resbP_kernel(
             )
 
         def round_pass(a):
-            for r0, r1 in WU_LOADS[a]:
-                cut = r0 + (r1 - r0) * SCALAR_EIGHTHS_OF_WU[a] // 8 if r1 == R else r1
-                round_wu(nc.scalar.copy, a, r0, r0, cut)
-                if cut < r1:
-                    round_wu(nc.vector.tensor_copy, a, r0, cut, r1)
+            cut = R * SCALAR_EIGHTHS_OF_WU[a] // 8
+            round_wu(nc.scalar.copy, a, 0, cut)
+            round_wu(nc.vector.tensor_copy, a, cut, R)
 
         round_pass(0)
         quantise_wu(0, 0, PACK)
-        gather_words(1, 0, J - LATE_GATHER, "wu_bf0")
         round_pass(1)
-        quantise_wu(1, 0, PACK // 2)
-        quantise_wu(1, PACK // 2, PACK)
-        gather_words(1, J - LATE_GATHER, J, offset=ROUNDED_WU)
+        quantise_wu(1, 0, PACK)
+        for j0, j1 in LATE_GATHERS:
+            gather_words(1, j0, j1)
         deal(nc.scalar.copy, wd8[:].bitcast(U32), wd8_raw[:].bitcast(U32))
-        deal(nc.vector.tensor_copy, wd4[:].bitcast(U16), wd4_raw[:].bitcast(U16))
-        wd_sc = sb("wd_sc", [P, N], U8, offset=ROUNDED_WU + 4 * LATE_GATHER)
-        deal(nc.vector.tensor_copy, wd_sc[:], wd_sc_raw[:])
 
         narrow = [bank_tile("narrow%d" % c, [P, PACK, NARROW], c) for c in range(HALF // NARROW)]
 
@@ -215,7 +207,7 @@ def tile_list_modp_silu_res_resbP_kernel(
         for t in range(WIDE_AHEAD):
             up_pass(wide[t][:], 0, t, HALF, J, True, False)
 
-        h_q = [sb("h_q%d" % u, [P, HALF], U32, tag="" if u else "wd_sc_raw") for u in range(2)]
+        h_q = [sb("h_q%d" % u, [P, HALF], U32) for u in range(2)]
         h_s = [sb("h_s%d" % u, [P, HALF], U8) for u in range(2)]
 
         def quantise_hidden(j0, j1, h_bf):
@@ -230,7 +222,7 @@ def tile_list_modp_silu_res_resbP_kernel(
             h_bf = sb("h_bf%d" % j0, [P, j1 - j0, PACK], BF16, offset=offset)
             for c in range(j0 // NARROW, j1 // NARROW):
                 up_narrow(1, c, False)
-                act = sb("act%d" % c, [P, NARROW, PACK], F32, offset={0: RAW_WD, 3: LAST_ACT}.get(c))
+                act = sb("act%d" % c, [P, NARROW, PACK], F32, offset={0: RAW_WD, 2: RAW_WD + 4 * N, 3: LAST_ACT}.get(c))
                 step = NARROW if c else NARROW // 2
                 for lo in range(0, NARROW, step):
                     part = act[:, lo : lo + step, :]
@@ -241,22 +233,22 @@ def tile_list_modp_silu_res_resbP_kernel(
                     )
             return h_bf[:]
 
-        def hidden_wide(j0, j1):
+        def hidden_wide(j0, j1, midway):
             width = j1 - j0
             act = [sb("act_slice%d" % t, [P, width], F32, offset=LAST_ACT - 2 * N if t == 1 else None) for t in range(PACK)]
             h_slices = sb("h_slices", [P, PACK, width], BF16, offset=LAST_ACT + 2 * N)
             h_bf = sb("h_bf%d" % j0, [P, width, PACK], BF16)
             for t in range(PACK):
-                cut = width - LATE_GATHER
                 ahead = t < WIDE_AHEAD
                 if not ahead:
                     wide[t] = bank_tile("wide", [P, width], LATE_BANKS[t])
-                up_pass(wide[t][:, 0:cut], 1, t, j0, j0 + cut, not ahead, False)
-                up_pass(wide[t][:, cut:width], 1, t, j0 + cut, j1, False, ahead)
+                up_pass(wide[t][:], 1, t, j0, j1, not ahead, ahead)
                 if not ahead:
                     up_pass(wide[t][:], 0, t, j0, j1, False, True)
                 nc.scalar.activation(act[t][:], wide[t][:], ACT.Silu)
                 nc.scalar.activation(h_slices[:, t, :], act[t][:], ACT.Copy, scale=sm_sb[:, t : t + 1])
+                if t == 1:
+                    midway()
             nc.scalar.copy(
                 out=h_bf[:].rearrange("p (c i) t -> p c t i", i=4),
                 in_=h_slices[:].rearrange("p t (c i) -> p c t i", i=4),
@@ -264,13 +256,12 @@ def tile_list_modp_silu_res_resbP_kernel(
             return h_bf[:]
 
         pieces = ((0, QUARTER), (QUARTER, HALF), (HALF, J))
-        units = [(t, j0, j1) for j0, j1 in pieces for t in (first, second)]
-        units = units + [(third, 0, J), (last, 0, J)]
-        held = (second, QUARTER)
-        y_sb = {(t, j0): sb("y_sb%d_%d" % (t, j0), [P, j1 - j0], F32) for t, j0, j1 in units if (t, j0) != held}
+        held = ((second, QUARTER), (third, QUARTER))
+        y_parts = [(t, j0, j1) for t in (first, second, third) for j0, j1 in pieces] + [(last, 0, J)]
+        y_sb = {(t, j0): sb("y_sb%d_%d" % (t, j0), [P, j1 - j0], F32) for t, j0, j1 in y_parts if (t, j0) not in held}
 
         def y_view(t, j0, j1):
-            base = j0 if (t, j0) in y_sb else 0
+            base = max(start for slice_t, start in y_sb if slice_t == t and start <= j0)
             return y_sb[t, base][:, j0 - base : j1 - base]
 
         def down(t, j0, j1, bank_index):
@@ -296,49 +287,63 @@ def tile_list_modp_silu_res_resbP_kernel(
                 )
             nc.scalar.activation(y_view(t, j0, j1), bank[:], ACT.Identity, bias=b_sb[:, t : t + 1])
 
-        first_h = [hidden_narrow(0, NARROW, RAW_WD + 4 * N), hidden_narrow(NARROW, QUARTER)]
+        first_h = [hidden_narrow(0, NARROW, FIRST_H), hidden_narrow(NARROW, QUARTER)]
+        deal(nc.scalar.copy, wd4[:].bitcast(U16), wd4_raw[:].bitcast(U16))
+        wd_sc = sb("wd_sc", [P, N], U8, tag="got_w1_0")
+        deal(nc.vector.tensor_copy, wd_sc[:], wd_sc_raw[:])
         for c, h_bank in enumerate(first_h):
             quantise_hidden(c * NARROW, (c + 1) * NARROW, h_bank)
         down(first, 0, QUARTER, 6)
         down(second, 0, QUARTER, 7)
-        quantise_hidden(QUARTER, HALF, hidden_narrow(QUARTER, HALF, RAW_WD + 4 * N))
+        quantise_hidden(QUARTER, HALF, hidden_narrow(QUARTER, HALF, FIRST_H))
         down(first, QUARTER, HALF, 0)
-        quantise_hidden(HALF, J, hidden_wide(HALF, J))
-        y_sb[held] = sb("y_held", [P, QUARTER], F32, offset=LAST_ACT + 2 * N)
-        down(second, QUARTER, HALF, 1)
-        down(first, HALF, J, 2)
-        down(second, HALF, J, 3)
-        down(third, 0, HALF, 4)
-        down(third, HALF, J, 5)
-        down(last, 0, HALF, 6)
-        down(last, HALF, J, 7)
+        quantise_hidden(HALF, J, hidden_wide(HALF, J, lambda: down(third, 0, QUARTER, 1)))
+        for place, part in enumerate(held):
+            y_sb[part] = sb("y_held%d" % place, [P, QUARTER], F32, offset=LAST_ACT + 2 * N + 4 * QUARTER * place)
+        down(second, QUARTER, HALF, 2)
+        down(third, QUARTER, HALF, 3)
+        down(first, HALF, J, 4)
+        down(second, HALF, J, 5)
+        down(third, HALF, J, 6)
+        down(last, 0, HALF, 7)
+        down(last, HALF, J, 0)
 
         out_rows = out_0.rearrange("(p t) c -> p t c", t=PACK)
         woven = [sb("woven%d" % g, [P, c1 - c0, PACK], BF16) for g, (c0, c1) in enumerate(BLOCKS)]
-        ring = sb("ring", [P, SUMS_IN_FLIGHT, J], F32)
+        sums = {t: sb("sum%d" % t, [P, J], F32) for t in SLICE_ORDER}
 
-        def unit_sum(k):
-            place = k if k < 2 else (k + 1) % SUMS_IN_FLIGHT
-            return ring[:, place, 0 : units[k][2] - units[k][1]]
+        def unit_sum(t, j0, j1):
+            shift = QUARTER if (t, j0) == (first, QUARTER) else 0
+            return sums[t][:, j0 - shift : j1 - shift]
 
-        def add_residual(k):
-            t, j0, j1 = units[k]
-            nc.vector.tensor_tensor(unit_sum(k), res[t][:].indirect(listed(j0, j1)), y_view(t, j0, j1), ADD)
+        def add_residual(t, j0, j1):
+            nc.vector.tensor_tensor(unit_sum(t, j0, j1), res[t][:].indirect(listed(j0, j1)), y_view(t, j0, j1), ADD)
 
-        def scatter(k):
-            t, j0, j1 = units[k]
-            nc.vector.tensor_tensor(page[t][:].indirect(listed(j0, j1)), unit_sum(k), wgo_sb[:, j0:j1], MULT)
+        def scatter(t, j0, j1):
+            nc.vector.tensor_tensor(page[t][:].indirect(listed(j0, j1)), unit_sum(t, j0, j1), wgo_sb[:, j0:j1], MULT)
             if j1 == J:
                 nc.sync.dma_start(out=out_rows[:, t, :], in_=page[t][:])
                 if t != last:
                     for g, (c0, c1) in enumerate(BLOCKS):
                         nc.scalar.copy(out=woven[g][:, :, t], in_=page[t][:, c0:c1])
 
-        add_residual(0)
-        for k in range(len(units)):
-            if k + 1 < len(units):
-                add_residual(k + 1)
-            scatter(k)
+        for t in (first, second):
+            add_residual(t, 0, QUARTER)
+        for t in (first, second):
+            scatter(t, 0, QUARTER)
+        for t, j0 in ((first, 0), (second, QUARTER)):
+            add_residual(t, QUARTER, HALF)
+            add_residual(third, j0, j0 + QUARTER)
+            scatter(t, QUARTER, HALF)
+        add_residual(first, HALF, J)
+        add_residual(second, HALF, HALF + QUARTER)
+        scatter(first, HALF, J)
+        add_residual(second, HALF + QUARTER, J)
+        add_residual(third, HALF, J)
+        scatter(second, HALF, J)
+        add_residual(last, 0, J)
+        scatter(third, 0, J)
+        scatter(last, 0, J)
 
         out_q = [sb("out_q%d" % g, [P, c1 - c0], I32) for g, (c0, c1) in enumerate(BLOCKS)]
         out_s = sb("out_s", [P, T], U8)

@@ -63,12 +63,12 @@ def tile_list_modp_silu_res_resbP_kernel(
             return offsets[:, j0 // 16 : j1 // 16]
 
         warm_in = sb("warm_in", [P, 1], F32)
-        nc.vector.memset(warm_in[:], 0.0)
+        nc.gpsimd.memset(warm_in[:], 0.0)
         warm_out = sb("warm_out", [P, 1], F32)
         nc.scalar.activation(warm_out[:], warm_in[:], ACT.Silu)
 
         tab_sc = sb("tab_sc", [P, T], U8)
-        nc.gpsimd.memset(tab_sc[:].bitcast(I32), 0)
+        nc.vector.memset(tab_sc[:].bitcast(I32), 0)
         wd_sc_raw = sb("wd_sc_raw", [P, N], U8)
         nc.vector.memset(wd_sc_raw[:].bitcast(I32), 0)
 
@@ -123,14 +123,13 @@ def tile_list_modp_silu_res_resbP_kernel(
 
         page = {}
 
-        def clear_page(engine, early, late, cuts=()):
+        def clear_page(engine, early, late):
             tile = sb("page%d" % early, [P, T], F32)
-            for c0, c1 in zip((0,) + cuts, cuts + (T,)):
-                engine.memset(tile[:, c0:c1].bitcast(I32), 0)
+            engine.memset(tile[:].bitcast(I32), 0)
             page[early] = tile
             page[late] = tile
 
-        clear_page(nc.vector, first, third, (T // 2 - 1, T // 2))
+        clear_page(nc.vector, first, third)
         clear_page(nc.vector, second, last)
 
         wu_bf = [sb("wu_bf%d" % a, [P, PACK, P, PACK], BF16, offset=ROUNDED_WU) for a in range(2)]

@@ -344,7 +344,7 @@ def tile_list_modp_silu_res_resbP_kernel(
         scatter(third, 0, J)
         scatter(last, 0, J)
 
-        out_q = [sb("out_q%d" % g, [P, c1 - c0], I32) for g, (c0, c1) in enumerate(BLOCKS)]
+        out_q = sb("out_q", [P, T], I32)
         out_s = sb("out_s", [P, T], U8)
         words_out = out_1[0].rearrange("p t i -> p (t i)").bitcast(I32)
 
@@ -360,10 +360,11 @@ def tile_list_modp_silu_res_resbP_kernel(
             if g + 1 < len(BLOCKS):
                 round_last(g + 1)
             nc.vector.quantize_mx(
-                out=out_q[g][:].bitcast(FP8X4), scales=out_s[:, c0:c1],
+                out=out_q[:, c0:c1].bitcast(FP8X4), scales=out_s[:, c0:c1],
                 in_=woven[g][:].rearrange("p c t -> p (c t)"),
             )
-            nc.sync.dma_start(out=words_out[:, c0:c1], in_=out_q[g][:])
+            if c1 % BANK == 0:
+                nc.sync.dma_start(out=words_out[:, c1 - BANK : c1], in_=out_q[:, c1 - BANK : c1])
         for q in range(4):
             queue = nc.scalar if q % 2 else nc.sync
             queue.dma_start(

@@ -345,7 +345,7 @@ def tile_list_modp_silu_res_resbP_kernel(
         scatter(last, 0, J)
 
         out_q = sb("out_q", [P, T], I32)
-        out_s = sb("out_s", [P, T], U8)
+        out_s = sb("out_s", [P, BANK], U8)
         words_out = out_1[0].rearrange("p t i -> p (t i)").bitcast(I32)
 
         def round_last(g):
@@ -359,14 +359,18 @@ def tile_list_modp_silu_res_resbP_kernel(
         for g, (c0, c1) in enumerate(BLOCKS):
             if g + 1 < len(BLOCKS):
                 round_last(g + 1)
-            nc.vector.quantize_mx(
-                out=out_q[:, c0:c1].bitcast(FP8X4), scales=out_s[:, c0:c1],
-                in_=woven[g][:].rearrange("p c t -> p (c t)"),
-            )
+            step = c1 - c0 if g == 0 else QUARTER
+            for lo in range(c0, c1, step):
+                nc.vector.quantize_mx(
+                    out=out_q[:, lo : lo + step].bitcast(FP8X4),
+                    scales=out_s[4 * (lo // BANK) : P, lo % BANK : lo % BANK + step],
+                    in_=woven[g][:, lo - c0 : lo - c0 + step, :].rearrange("p c t -> p (c t)"),
+                )
             if c1 % BANK == 0:
                 nc.sync.dma_start(out=words_out[:, c1 - BANK : c1], in_=out_q[:, c1 - BANK : c1])
         for q in range(4):
             queue = nc.scalar if q % 2 else nc.sync
             queue.dma_start(
-                out=out_2[0, 4 * q : 4 * q + 4, :].bitcast(I32), in_=out_s[32 * q : 32 * q + 4, :].bitcast(I32)
+                out=out_2[0, 4 * q : 4 * q + 4, :].bitcast(I32).rearrange("i (j c) -> j i c", j=T // BANK),
+                in_=out_s[32 * q : 32 * q + 16, :].bitcast(I32),
             )

from contextlib import ExitStack

import concourse.mybir as mybir

K, R, N, T, J = 1024, 512, 512, 2048, 1024
FLOPS = 2 * K * R * J + 2 * 2 * R * N * J

F32 = mybir.dt.float32
BF16 = mybir.dt.bfloat16
I32 = mybir.dt.int32
U32 = mybir.dt.uint32
U16 = mybir.dt.uint16
U8 = mybir.dt.uint8
FP8X4 = mybir.dt.float8_e4m3fn_x4
FP4X4 = mybir.dt.float4_e2m1fn_x4
ACT = mybir.ActivationFunctionType
ADD = mybir.AluOpType.add
MULT = mybir.AluOpType.mult

P = 128
PACK = 4
BANK = 512
NARROW = BANK // PACK
HALF = J // 2
QUARTER = J // 4
SLICE_ORDER = (0, 2, 1, 3)
BLOCKS = ((0, 512), (512, 1024), (1024, 1536), (1536, 1792), (1792, 2048))
SCALAR_EIGHTHS_OF_WU = (5, 3)
TABLE_LEAD = 256
LATE_GATHERS = ((0, 128), (128, 256), (256, 512), (512, 1024))
WIDE_AHEAD = 1
LATE_BANKS = {1: 5, 2: 6, 3: 7}
RAW_WD = 0
ROUNDED_WU = RAW_WD + 8 * N
LAST_ACT = ROUNDED_WU + 10 * N
FIRST_H = LAST_ACT + 10 * N
VECTOR_EIGHTHS_OF_BLOCK = 5


def tile_list_modp_silu_res_resbP_kernel(
    tc, tab_words, tab_scales, wu, sm, wd4_words, wd4_scales, wd8_words, wd8_scales, rT, b, wgo, offs,
    out_0, out_1, out_2,
):
    nc = tc.nc
    first, second, third, last = SLICE_ORDER
    with ExitStack() as ctx:
        keep = ctx.enter_context(tc.tile_pool(name="keep", bufs=1))
        placed = ctx.enter_context(tc.tile_pool(name="placed", bufs=1))
        psum = ctx.enter_context(tc.psum_pool(name="psum", bufs=1))

        def sb(name, shape, dtype, tag="", offset=None):
            if offset is not None:
                return placed.tile(shape, dtype, name=name, offset=offset, align_bytes=64)
            return keep.tile(shape, dtype, name=name, tag=tag or name, align_bytes=64)

        def bank_tile(name, shape, bank):
            return psum.tile(shape, F32, name=name, tag="bank%d" % bank)

        offsets = keep.tile([P, J // 16], U16, name="offsets")
        nc.sync.dma_start(offsets[:], offs)

        def listed(j0, j1):
            return offsets[:, j0 // 16 : j1 // 16]

        warm_in = sb("warm_in", [P, 1], F32)
        nc.gpsimd.memset(warm_in[:], 0.0)
        warm_out = sb("warm_out", [P, 1], F32)
        nc.scalar.activation(warm_out[:], warm_in[:], ACT.Silu)

        tab_sc = sb("tab_sc", [P, T], U8)
        nc.vector.memset(tab_sc[:].bitcast(I32), 0)
        wd_sc_raw = sb("wd_sc_raw", [P, N], U8)
        nc.vector.memset(wd_sc_raw[:].bitcast(I32), 0)

        tab_w = [sb("tab_w%d" % a, [P, T], I32) for a in range(2)]
        wu_raw = [sb("wu_raw%d" % a, [P, PACK, R], F32) for a in range(2)]

        def load_wu(a):
            rows = wu[512 * a : 512 * (a + 1), :].rearrange("(p i) r -> p i r", i=PACK)
            nc.sync.dma_start(out=wu_raw[a][:], in_=rows)

        def load_table(a, c0, c1):
            words = tab_words[a].rearrange("p t i -> p (t i)").bitcast(I32)
            nc.sync.dma_start(out=tab_w[a][:, c0:c1], in_=words[:, c0:c1])

        def load_wd_scales(queue, tier, scales):
            for q in range(4):
                first_row = 32 * q + 4 * tier
                queue.dma_start(
                    out=wd_sc_raw[first_row : first_row + 4, :].bitcast(I32),
                    in_=scales[0, 4 * q : 4 * q + 4, :].bitcast(I32),
                )

        load_table(0, 0, TABLE_LEAD)
        for q in range(4):
            nc.sync.dma_start(
                out=tab_sc[32 * q : 32 * q + 8, :].bitcast(I32),
                in_=tab_scales[:, 4 * q : 4 * q + 4, :].bitcast(I32),
            )
        load_table(0, TABLE_LEAD, T)
        load_wu(0)
        load_wd_scales(nc.gpsimd, 0, wd4_scales)
        load_wd_scales(nc.sync, 1, wd8_scales)
        load_wu(1)
        load_table(1, 0, T)
        wd8_raw = sb("wd8_raw", [P, N], I32, offset=RAW_WD)
        nc.sync.dma_start(out=wd8_raw[:], in_=wd8_words[0].rearrange("p n i -> p (n i)").bitcast(I32))
        wd4_raw = sb("wd4_raw", [P, 2 * N], U8, offset=RAW_WD + 4 * N)
        nc.sync.dma_start(out=wd4_raw[:].bitcast(I32), in_=wd4_words[0].bitcast(I32))
        sm_sb = sb("sm_sb", [P, PACK], F32)
        nc.sync.dma_start(out=sm_sb[:], in_=sm.rearrange("(p t) -> p t", t=PACK))
        b_sb = sb("b_sb", [P, PACK], F32)
        nc.sync.dma_start(out=b_sb[:], in_=b.rearrange("(p t) -> p t", t=PACK))
        res = {t: sb("res%d" % t, [P, T], F32) for t in SLICE_ORDER}
        res_rows = rT.rearrange("(p t) c -> p t c", t=PACK)
        wgo_sb = sb("wgo_sb", [P, J], F32)
        nc.sync.dma_start(out=res[first][:], in_=res_rows[:, first, :])
        nc.sync.dma_start(out=res[second][:], in_=res_rows[:, second, :])
        nc.sync.dma_start(out=wgo_sb[:, 0:QUARTER], in_=wgo[:, 0:QUARTER])
        nc.sync.dma_start(out=res[third][:], in_=res_rows[:, third, :])
        nc.sync.dma_start(out=wgo_sb[:, QUARTER:J], in_=wgo[:, QUARTER:J])
        nc.sync.dma_start(out=res[last][:], in_=res_rows[:, last, :])

        page = {}

        def clear_page(engine, early, late):
            tile = sb("page%d" % early, [P, T], F32)
            engine.memset(tile[:].bitcast(I32), 0)
            page[early] = tile
            page[late] = tile

        clear_page(nc.vector, first, third)
        clear_page(nc.vector, second, last)

        wu_bf = [sb("wu_bf%d" % a, [P, PACK, P, PACK], BF16, offset=ROUNDED_WU) for a in range(2)]
        wu_q = [sb("wu_q%d" % a, [P, R], U32) for a in range(2)]
        wu_s = [sb("wu_s%d" % a, [P, R], U8) for a in range(2)]

        def round_wu(copy, a, r0, r1):
            copy(
                out=wu_bf[a][:, :, r0 // PACK : r1 // PACK, :].rearrange("p t m i -> p m i t"),
                in_=wu_raw[a][:, :, r0:r1].rearrange("p i (m t) -> p m i t", t=PACK),
            )

        wd8 = sb("wd8", [P, N], I32)
        wd4 = sb("wd4", [P, 2 * N], U8)

        def deal(copy, out, in_):
            copy(out=out.rearrange("p (t m) -> p m t", t=PACK), in_=in_.rearrange("p (m t) -> p m t", t=PACK))

        got_w = {}

        def gather_words(a, j0, j1):
            tile = sb("got_w%d_%d" % (a, j0), [P, j1 - j0], U32)
            nc.vector.tensor_copy(tile[:], tab_w[a][:].bitcast(U32).indirect(listed(j0, j1)))
            for j in range(j0, j1, NARROW):
                got_w[a, j] = (tile, j0)

        def up_pass(out, a, t, j0, j1, start, stop):
            tile, base = got_w[a, j0]
            nc.tensor.matmul_mx(
                out=out,
                lhsT=wu_q[a][:, t * P : (t + 1) * P].bitcast(FP8X4),
                lhsT_scale=wu_s[a][:, t * P : (t + 1) * P],
                rhs=tile[:, j0 - base : j1 - base].bitcast(FP8X4),
                rhs_scale=got_sc[4 * a : P, j0:j1],
                start=start, stop=stop,
            )

        got_sc = sb("got_sc", [P, J], U8)
        nc.vector.tensor_copy(got_sc[:], tab_sc[:].indirect(offsets[:]))
        gather_words(0, 0, J)

        def quantise_wu(a, t0, t1):
            cols = slice(t0 * P, t1 * P)
            nc.vector.quantize_mx(
                out=wu_q[a][:, cols].bitcast(FP8X4), scales=wu_s[a][:, cols],
                in_=wu_bf[a][:, t0:t1, :, :].rearrange("p t m i -> p (t m i)"),
            )

        def round_pass(a):
            cut = R * SCALAR_EIGHTHS_OF_WU[a] // 8
            round_wu(nc.scalar.copy, a, 0, cut)
            round_wu(nc.vector.tensor_copy, a, cut, R)

        round_pass(0)
        quantise_wu(0, 0, PACK)
        round_pass(1)
        quantise_wu(1, 0, PACK)
        for j0, j1 in LATE_GATHERS:
            gather_words(1, j0, j1)
        deal(nc.scalar.copy, wd8[:].bitcast(U32), wd8_raw[:].bitcast(U32))

        narrow = [bank_tile("narrow%d" % c, [P, PACK, NARROW], c) for c in range(HALF // NARROW)]

        def up_narrow(a, c, opens):
            for t in range(PACK):
                up_pass(
                    narrow[c][:, t, :], a, t, c * NARROW, (c + 1) * NARROW,
                    opens and t == 0, not opens and t == PACK - 1,
                )

        for c in range(len(narrow)):
            up_narrow(0, c, True)
        wide = {t: bank_tile("wide", [P, HALF], PACK + t) for t in range(WIDE_AHEAD)}
        for t in range(WIDE_AHEAD):
            up_pass(wide[t][:], 0, t, HALF, J, True, False)

        h_q = [sb("h_q%d" % u, [P, HALF], U32) for u in range(2)]
        h_s = [sb("h_s%d" % u, [P, HALF], U8) for u in range(2)]

        def quantise_hidden(j0, j1, h_bf):
            u = j0 // HALF
            cols = slice(j0 - u * HALF, j1 - u * HALF)
            nc.vector.quantize_mx(
                out=h_q[u][:, cols].bitcast(FP8X4), scales=h_s[u][:, cols],
                in_=h_bf.rearrange("p j t -> p (j t)"),
            )

        def hidden_narrow(j0, j1, offset=None):
            h_bf = sb("h_bf%d" % j0, [P, j1 - j0, PACK], BF16, offset=offset)
            for c in range(j0 // NARROW, j1 // NARROW):
                up_narrow(1, c, False)
                act = sb("act%d" % c, [P, NARROW, PACK], F32, offset={0: RAW_WD, 2: RAW_WD + 4 * N, 3: LAST_ACT}.get(c))
                step = NARROW if c else NARROW // 2
                for lo in range(0, NARROW, step):
                    part = act[:, lo : lo + step, :]
                    nc.scalar.activation(part, narrow[c][:, :, lo : lo + step].rearrange("p t j -> p j t"), ACT.Silu)
                    nc.vector.tensor_tensor(
                        h_bf[:, c * NARROW - j0 + lo : c * NARROW - j0 + lo + step, :], part,
                        sm_sb[:].unsqueeze(1).to_broadcast([P, step, PACK]), MULT,
                    )
            return h_bf[:]

        def hidden_wide(j0, j1, midway):
            width = j1 - j0
            act = [sb("act_slice%d" % t, [P, width], F32, offset=LAST_ACT - 2 * N if t == 1 else None) for t in range(PACK)]
            h_slices = sb("h_slices", [P, PACK, width], BF16, offset=LAST_ACT + 2 * N)
            h_bf = sb("h_bf%d" % j0, [P, width, PACK], BF16)
            for t in range(PACK):
                ahead = t < WIDE_AHEAD
                if not ahead:
                    wide[t] = bank_tile("wide", [P, width], LATE_BANKS[t])
                up_pass(wide[t][:], 1, t, j0, j1, not ahead, ahead)
                if not ahead:
                    up_pass(wide[t][:], 0, t, j0, j1, False, True)
                nc.scalar.activation(act[t][:], wide[t][:], ACT.Silu)
                nc.scalar.activation(h_slices[:, t, :], act[t][:], ACT.Copy, scale=sm_sb[:, t : t + 1])
                if t == 1:
                    midway()
            nc.scalar.copy(
                out=h_bf[:].rearrange("p (c i) t -> p c t i", i=4),
                in_=h_slices[:].rearrange("p t (c i) -> p c t i", i=4),
            )
            return h_bf[:]

        pieces = ((0, QUARTER), (QUARTER, HALF), (HALF, J))
        held = ((second, QUARTER), (third, QUARTER))
        y_parts = [(t, j0, j1) for t in (first, second, third) for j0, j1 in pieces] + [(last, 0, J)]
        y_sb = {(t, j0): sb("y_sb%d_%d" % (t, j0), [P, j1 - j0], F32) for t, j0, j1 in y_parts if (t, j0) not in held}

        def y_view(t, j0, j1):
            base = max(start for slice_t, start in y_sb if slice_t == t and start <= j0)
            return y_sb[t, base][:, j0 - base : j1 - base]

        def down(t, j0, j1, bank_index):
            u = j0 // HALF
            width = j1 - j0
            step = BANK if width == BANK else NARROW
            bank = bank_tile("down", [P, width], bank_index)
            for c0 in range(0, width, step):
                cols = slice(j0 - u * HALF + c0, j0 - u * HALF + c0 + step)
                nc.tensor.matmul_mx(
                    out=bank[:, c0 : c0 + step],
                    lhsT=wd4[:, 2 * t * P : 2 * (t + 1) * P].bitcast(FP4X4),
                    lhsT_scale=wd_sc[:, t * P : (t + 1) * P],
                    rhs=h_q[u][:, cols].bitcast(FP8X4), rhs_scale=h_s[u][:, cols],
                    start=True, stop=False,
                )
                nc.tensor.matmul_mx(
                    out=bank[:, c0 : c0 + step],
                    lhsT=wd8[:, t * P : (t + 1) * P].bitcast(FP8X4),
                    lhsT_scale=wd_sc[4:P, t * P : (t + 1) * P],
                    rhs=h_q[u][:, cols].bitcast(FP8X4), rhs_scale=h_s[u][:, cols],
                    start=False, stop=True,
                )
            nc.scalar.activation(y_view(t, j0, j1), bank[:], ACT.Identity, bias=b_sb[:, t : t + 1])

        first_h = [hidden_narrow(0, NARROW, FIRST_H), hidden_narrow(NARROW, QUARTER)]
        deal(nc.scalar.copy, wd4[:].bitcast(U16), wd4_raw[:].bitcast(U16))
        wd_sc = sb("wd_sc", [P, N], U8, tag="got_w1_0")
        deal(nc.vector.tensor_copy, wd_sc[:], wd_sc_raw[:])
        for c, h_bank in enumerate(first_h):
            quantise_hidden(c * NARROW, (c + 1) * NARROW, h_bank)
        down(first, 0, QUARTER, 6)
        down(second, 0, QUARTER, 7)
        quantise_hidden(QUARTER, HALF, hidden_narrow(QUARTER, HALF, FIRST_H))
        down(first, QUARTER, HALF, 0)
        quantise_hidden(HALF, J, hidden_wide(HALF, J, lambda: down(third, 0, QUARTER, 1)))
        for place, part in enumerate(held):
            y_sb[part] = sb("y_held%d" % place, [P, QUARTER], F32, offset=LAST_ACT + 2 * N + 4 * QUARTER * place)
        down(second, QUARTER, HALF, 2)
        down(third, QUARTER, HALF, 3)
        down(first, HALF, J, 4)
        down(second, HALF, J, 5)
        down(third, HALF, J, 6)
        down(last, 0, HALF, 7)
        down(last, HALF, J, 0)

        out_rows = out_0.rearrange("(p t) c -> p t c", t=PACK)
        woven = [sb("woven%d" % g, [P, c1 - c0, PACK], BF16) for g, (c0, c1) in enumerate(BLOCKS)]
        sums = {t: sb("sum%d" % t, [P, J], F32) for t in SLICE_ORDER}

        def unit_sum(t, j0, j1):
            shift = QUARTER if (t, j0) == (first, QUARTER) else 0
            return sums[t][:, j0 - shift : j1 - shift]

        def add_residual(t, j0, j1):
            nc.vector.tensor_tensor(unit_sum(t, j0, j1), res[t][:].indirect(listed(j0, j1)), y_view(t, j0, j1), ADD)

        def scatter(t, j0, j1):
            nc.vector.tensor_tensor(page[t][:].indirect(listed(j0, j1)), unit_sum(t, j0, j1), wgo_sb[:, j0:j1], MULT)
            if j1 == J:
                nc.sync.dma_start(out=out_rows[:, t, :], in_=page[t][:])
                if t != last:
                    for g, (c0, c1) in enumerate(BLOCKS):
                        nc.scalar.copy(out=woven[g][:, :, t], in_=page[t][:, c0:c1])

        for t in (first, second):
            add_residual(t, 0, QUARTER)
        for t in (first, second):
            scatter(t, 0, QUARTER)
        for t, j0 in ((first, 0), (second, QUARTER)):
            add_residual(t, QUARTER, HALF)
            add_residual(third, j0, j0 + QUARTER)
            scatter(t, QUARTER, HALF)
        add_residual(first, HALF, J)
        add_residual(second, HALF, HALF + QUARTER)
        scatter(first, HALF, J)
        add_residual(second, HALF + QUARTER, J)
        add_residual(third, HALF, J)
        scatter(second, HALF, J)
        add_residual(last, 0, J)
        scatter(third, 0, J)
        scatter(last, 0, J)

        out_q = sb("out_q", [P, T], I32)
        out_s = sb("out_s", [P, BANK], U8)
        words_out = out_1[0].rearrange("p t i -> p (t i)").bitcast(I32)

        def round_last(g):
            c0, c1 = BLOCKS[g]
            share = (c1 - c0) * VECTOR_EIGHTHS_OF_BLOCK // 8 if c1 - c0 == BANK else 0
            if share:
                nc.vector.tensor_copy(woven[g][:, 0:share, last], page[last][:, c0 : c0 + share])
            nc.scalar.copy(out=woven[g][:, share : c1 - c0, last], in_=page[last][:, c0 + share : c1])

        round_last(0)
        for g, (c0, c1) in enumerate(BLOCKS):
            if g + 1 < len(BLOCKS):
                round_last(g + 1)
            step = c1 - c0 if g == 0 else QUARTER
            for lo in range(c0, c1, step):
                nc.vector.quantize_mx(
                    out=out_q[:, lo : lo + step].bitcast(FP8X4),
                    scales=out_s[4 * (lo // BANK) : P, lo % BANK : lo % BANK + step],
                    in_=woven[g][:, lo - c0 : lo - c0 + step, :].rearrange("p c t -> p (c t)"),
                )
            if c1 % BANK == 0:
                nc.sync.dma_start(out=words_out[:, c1 - BANK : c1], in_=out_q[:, c1 - BANK : c1])
        for q in range(4):
            queue = nc.scalar if q % 2 else nc.sync
            queue.dma_start(
                out=out_2[0, 4 * q : 4 * q + 4, :].bitcast(I32).rearrange("i (j c) -> j i c", j=T // BANK),
                in_=out_s[32 * q : 32 * q + 16, :].bitcast(I32),
            )
